import numpy as np, ml_dtypes
CORES = [16,17,18,19,32,33,34,35]
N = 8
BF = ml_dtypes.bfloat16
def gentries(a):
    return np.ascontiguousarray(a.reshape(8, 16, -1).transpose(0, 2, 1)).reshape(8, -1)
def gtable(e):
    e = np.asarray(e); return np.ascontiguousarray(e.reshape(8, -1, 16).transpose(0, 2, 1)).reshape(128, -1).astype(np.int32)
V, G, NB, RO, HP = 1024, 512, 2, 4, 2
H = NB * G
S = V + H
def vals(rng, n):
    p = rng.choice(np.array([0.5, 1.0, 1.0, 2.0]), (N, 8, 1, n)) * rng.choice(np.array([0.7, 1.0, 1.4]), (N, 8, 16, 1))
    return np.minimum((256 * rng.random((N, 8, 16, n)) ** p).astype(np.int64), 255)
def parts(rng):
    m = rng.choice(np.array([2, 4, 16, 16]), (N, 8, 1, V))
    e = np.take_along_axis(rng.integers(0, S, (N, 8, 16, V)), (rng.random((N, 8, 16, V)) * m).astype(np.int64), axis=2)
    share = np.where(rng.random((N, 8, 1, V)) < 0.03125, 1.0, rng.choice(np.array([0.0, 0.0, 0.1, 0.3]), (N, 8, 1, V)))
    e = e + S * (rng.random((N, 8, 16, V)) < share)
    u = rng.integers(0, 16 * V, (N, 8, 16, V)); s = rng.integers(0, V // 4, (N, 8, H))
    h = rng.choice(np.array([200, 600, 1000, 1300, 1600]), (N, 8, RO)) + rng.integers(0, 200, (N, 8, RO))
    return e, u, vals(rng, V), vals(rng, V), vals(rng, S), s, h
def pack(e, u, x, b, y, s, h):
    flat = lambda a: np.ascontiguousarray(a.reshape(N, 128, a.shape[-1]))
    return {"ent": flat(e).astype(np.int32), "usr": flat(u).astype(np.int32), "xa": flat(x).astype(np.float32).astype(BF), "bn": flat(b).astype(np.float32).astype(BF),
            "yc": flat(y).astype(np.float32).astype(BF), "snd": np.stack([gtable(a) for a in s]), "th": np.ascontiguousarray(h).astype(np.int32)}
def setup_inputs(rng):
    return pack(*parts(rng))
def setup_inputs_spread(rng):
    e, u, x, b, y, s, h = parts(rng)
    def uneven(n):
        v = np.minimum((np.exp2(8 * rng.random((N, 8, 1, n))) * rng.random((N, 8, 16, n))).astype(np.int64), 255)
        return np.where(rng.random((N, 8, 1, n)) < 0.5, v, 255 - v)
    src = np.minimum((S * rng.random((N, 8, 16, V)) ** rng.choice(np.array([0.3, 1.0, 3.0]), (N, 8, 1, 1))).astype(np.int64), S - 1)
    e = src + S * (e >= S)
    w = np.minimum((V * rng.random((N, 8, 16, V)) ** rng.choice(np.array([0.5, 1.0, 2.0]), (N, 8, 1, 1))).astype(np.int64), V - 1)
    u = 16 * w + rng.integers(0, 16, (N, 8, 16, V))
    h = np.minimum(np.exp2(12 * rng.random((N, 8, RO))).astype(np.int64) - 1, 4080)
    return pack(e, u, uneven(V), uneven(V), uneven(S), s, h)
def setup_inputs_ends(rng):
    def two(n):
        mode = rng.integers(0, 3, (N, 8, 1, n)); bits = rng.integers(0, 2, (N, 8, 16, n))
        return 255 * np.where(mode == 0, 0, np.where(mode == 1, 1, bits))
    def mix(top, share, other):
        return np.where(rng.random((N, 8, 16, V)) < share, top * rng.integers(0, 2, (N, 8, 16, V)), other)
    x, b, y = two(V), two(V), two(S); v = np.arange(V)
    near = rng.choice(np.array([0, V - 1, V, S - 1, S, S + V - 1, S + V]), (N, 8, 16, V))
    e = mix(2 * S - 1, 0.75, np.where(rng.random((N, 8, 16, V)) < 0.5, near, rng.integers(0, 2 * S, (N, 8, 16, V))))
    u = mix(16 * V - 1, 0.75, rng.integers(0, 16 * V, (N, 8, 16, V)))
    none = v % 8 == 2; one = rng.integers(0, 16, (N, 8, 1, V))
    e = np.where(none, 2 * S - 1, np.where(np.arange(16)[:, None] == one, 0, e))
    top = np.where(np.arange(8) % 2 == 0, 255, 0)[None, :, None]
    x[:, :, :, 0] = top; y[:, :, :, 0] = top; b[:, :, :, 0] = 0; e[:, :, :, 0] = 0
    u[:, :4, 0, 0] = 0; u[:, 4:, 0, 0] = 16 * V - 1
    far = list(range(1, 8)) + list(range(V - 8, V))
    x[:, :, :, far] = 255 - top[..., None]; b[:, :, :, far] = 0; e[:, :, :, far] = 0; u[:, :, 0, far] = 16 * V - 1
    lone = list(range(12, 16)) + list(range(V - 12, V - 8))
    x[:, :, :, lone] = 255 - top[..., None]; e[:, :, :15, lone] = 2 * S - 1; e[:, :, 15, lone] = 0
    still = list(range(8, 12))
    x[:, :, :, still] = top[..., None]; b[:, :, :, still] = 0; e[:, :, :, still] = 0; u[:, :, 0, still] = 0
    s = (V // 4 - 1) * rng.integers(0, 2, (N, 8, H))
    h = 4080 * rng.integers(0, 2, (N, 8, RO)); h[:, 0, 0] = 0; h[:, 1, 0] = 0; h[:, 6, 0] = 4080; h[:, 7, 0] = 4080; h[N - 1, :, 1] = 4080
    return pack(e, u, x, b, y, s, h)
def setup_inputs_corners(rng):
    e, u, x, b, y, s, h = parts(rng); v = np.arange(V)
    src = rng.integers(0, S, (N, 8, 16, V)); src[:, 3] = v; src[:, 5] = rng.integers(V, S, (N, 16, V))
    src[:, 6] = rng.choice(np.array([0, V - 1, V, S - 1]), (N, 16, V))
    cl = rng.choice(np.array([0, 1, 2, 15, 16]), (N, 8, 1, V)); cl[:, 5] = 16
    o = np.argsort(rng.random((N, 8, 16, V)), axis=2); o[:, 0] = np.arange(15, -1, -1)[:, None]; o[:, 7] = np.arange(16)[:, None]
    gone = o >= cl; gone[:, 4, 15] = True
    q = rng.integers(0, 16, (N, 8, 16, V))
    u[:, 1] = 16 * np.where(v < V // 2, v, v ^ 1) + q[:, 1]; u[:, 2] = 16 * ((v + 1) % V) + q[:, 2]
    u[:, 3] = 16 * rng.choice(np.array([0, V - 1]), (N, 16, V)) + q[:, 3]; u[:, 4] = 16 * (u[:, 4] >> 4) + 15
    e = src + S * gone
    for a in range(N):
        turn = np.roll(np.arange(8), a); e[a] = e[a][turn]; u[a] = u[a][turn]
    e[1, :, :, 2::4] = e[1, :, :, 2::4] % S + S
    s[:, ::2] = rng.choice(np.array([0, V // 4 - 1]), (N, 4, H))
    h = rng.choice(np.array([0, 1, 300, 1000, 1400, 4079, 4080]), (N, 8, RO))
    return pack(e, u, x, b, y, s, h)
def setup_inputs_limits(rng):
    e, u, x, b, y, s, h = parts(rng); m = V // 4; a = np.arange(N)[:, None]; g = np.arange(8)[None, :]; k = np.arange(16)[:, None]; p = rng.permutation(N)
    base = np.where((a + g) % 2 == 0, rng.integers(2048, 3824, (N, 8)), rng.integers(64, 1700, (N, 8)))
    eff = base[..., None] + np.argsort(rng.random((N, 8, m)), axis=2)
    d = (eff[:, :, None] + np.argsort(rng.random((N, 8, 16, m)), axis=2)) // 16
    mv = (rng.random((N, 8, 8, m)) * (np.minimum(255 - d[:, :, :8], d[:, :, 8:]) + 1)).astype(np.int64)
    d = np.concatenate([d[:, :, :8] + mv, d[:, :, 8:] - mv], axis=2)
    fv = (rng.random(d.shape) * (np.minimum(128, 255 - d) + 1)).astype(np.int64)
    x[..., 3::4] = np.where((fv >= d) & (rng.random(d.shape) < 0.5), fv - d, fv + d)
    b[..., 3::4] = np.where((fv < 128) & (rng.random(d.shape) < 0.5), 127 - fv, 127 + fv)
    w = 4 * np.argsort(rng.random((N, 8, 4, m)), axis=3) + 3
    u = 16 * w.transpose(0, 1, 3, 2).reshape(N, 8, 1, V) + rng.integers(8, 16, (N, 8, 16, V))
    e = np.where(k == rng.integers(0, 16, (N, 8, 1, V)), e % S, e)
    o = np.argsort(rng.random((N, 8, S)), axis=2); lo, hi = o[..., 0], o[..., 1]
    y[a, g, :, lo] = 0; y[a, g, :, hi] = 255; lo = lo[..., None]; hi = hi[..., None]
    c = rng.integers(0, 2, (N, 8, m)) == 1
    e[..., 3::4] = e[..., 3::4] % S + S * (k < 8)
    e[:, :, 0, 3::4] = S + np.where(c, lo, hi); e[:, :, 7, 3::4] = S + np.where(c, hi, lo)
    h = base[..., None] + rng.integers(32, m - 64, (N, 8, RO))
    h = h - (h & 15) + rng.choice(np.array([0, 1, 2, 3, 4, 5, 10, 11, 12, 13, 14, 15]), h.shape)
    h[p[:2], :, 0] = 4080; h[p[2:], rng.integers(0, 8, N - 2), 0] = 4080; h[p[1], :, 1] = 0
    few = 4 * rng.permutation(m)[:int(rng.integers(1, 32))]; ez = e[p[1], int(rng.integers(0, 8))]
    ez[:, few] = ez[:, few] % S + S
    e[p[1], ::2, :, 1::4] = e[p[1], ::2, :, 1::4] % S + S
    return pack(e, u, x, b, y, s, h)
def setup_inputs_ties(rng):
    e, u, x, b, y, s, h = parts(rng)
    base = rng.choice(np.array([0, 100, 252]), (N, 8, 1, 1)); base[:, 0] = 252; base[:, 7] = 0
    x = base + rng.integers(0, 4, (N, 8, 16, V)); y = base + rng.integers(0, 4, (N, 8, 16, S)); b = rng.integers(0, 4, (N, 8, 16, V))
    x[:, :, :, 1::4] = x[:, :, :, 0::4]; x[:, :, :, 3::4] = x[:, :, :, 2::4]
    h = rng.integers(0, 40, (N, 8, RO))
    return pack(e, u, x, b, y, s, h)
def check_inputs(d):
    bad = []
    for k, lo, hi in (("ent", 0, 2 * S - 1), ("usr", 0, 16 * V - 1), ("xa", 0, 255), ("bn", 0, 255), ("yc", 0, 255), ("snd", 0, V // 4 - 1), ("th", 0, 4080)):
        v = np.asarray(d[k]).astype(np.float64)
        if not np.all((v >= lo) & (v <= hi)): bad.append("range of " + k)
        elif np.any(v != np.floor(v)): bad.append("whole numbers of " + k)
    return bad
def mid(a, b):
    return np.abs(((np.maximum.reduce(a, axis=3) + np.minimum.reduce(a, axis=3)) >> 1) - b)
def nodes(a, dtype):
    return np.ascontiguousarray(np.asarray(a).astype(np.float32).astype(dtype).reshape(N, 8, 16, -1).transpose(0, 1, 3, 2))
def reference(ent, usr, xa, bn, yc, snd, th):
    e, u = nodes(ent, np.int64), nodes(usr, np.int64); x, b, y = nodes(xa, np.int32), nodes(bn, np.int32), nodes(yc, np.int32)
    sl = np.stack([gentries(a) for a in snd]).astype(np.int64).reshape(N, 8, NB, 4, G // 4) * 4 + np.arange(4)[:, None]
    sl = sl.reshape(N, 8, NB, G); hh = th.astype(np.int64)
    r3 = np.arange(N)[:, None, None]; g3 = np.arange(8)[None, :, None]; r4 = r3[..., None]; g4 = g3[..., None]; sixteen = np.arange(16)
    gone = np.zeros(N, np.int64)
    for t in range(RO):
        w = [x]
        for n in range(1, NB + 1):
            q = (np.arange(N) + n) % N
            w.append(x[q][r3, g3, sl[q, :, n - 1]])
        w = np.concatenate(w + [y], axis=2)
        own = np.arange(t % 4, V, 4)
        eo = e[:, :, own]; xo = x[:, :, own]; bo = b[:, :, own]
        src = w[r4, g4, eo]
        score = np.add.reduce(np.abs(src - xo[:, :, :, None]), axis=4); clean = eo < S; some = np.any(clean, axis=3)
        k = np.argmin(np.where(clean, score, 9999), axis=3)
        hit = (sixteen == k[..., None]) & some[..., None]
        ek = np.take_along_axis(eo, k[..., None], 3)[..., 0]
        cv = w[r3, g3, np.where(some, ek + S, 0)]
        f0 = mid(src, bo); z = mid(np.where(hit[..., None], cv[:, :, :, None], src), bo); z0 = z
        c = np.broadcast_to(own, some.shape); dead = np.zeros(some.shape, bool)
        for hop in range(HP):
            p = u[r3, g3, c, np.add.reduce(z, axis=3) & 15]
            c = p >> 4; at = sixteen == (p & 15)[..., None]; ew = e[r3, g3, c]
            dead = dead | np.any(at & (ew >= S), axis=3)
            z = mid(np.where(at[..., None], z[:, :, :, None], w[r4, g4, ew]), b[r3, g3, c])
        D = np.where(dead, 0, np.add.reduce(np.abs(z - x[r3, g3, c]), axis=3))
        stay = some & (D <= hh[:, :, t][..., None] + (gone & 31)[:, None, None])
        e[:, :, own] = np.where(stay[..., None] & hit, eo + S, eo)
        x[:, :, own] = np.where(stay[..., None], z0, f0)
        gone = np.add.reduce(stay.astype(np.int64), axis=(1, 2))
    return {"ye": np.ascontiguousarray(e.transpose(0, 1, 3, 2)).reshape(N, 128, V).astype(np.float32), "yx": np.ascontiguousarray(x.transpose(0, 1, 3, 2)).reshape(N, 128, V).astype(np.float32).astype(BF)}

@@ -1,0 +1,691 @@
+import numpy as np
+from concourse.bass import DstId, RemoteDMATransfer
+from concourse.mybir import AluOpType as A, AxisListType, ActivationFunctionType as F
+
+V, NCL, RO = 1024, 4, 4
+WINW = 4096 + 128
+MAGIC = 12582912.0
+
+SCRATCH = {
+    "EI": ("sbuf", [128, 1024], "int32"), "EE": ("sbuf", [128, 1024], "float32"), "UI": ("sbuf", [128, 1024], "int32"),
+    "UT": ("sbuf", [128, 1024], "int32"), "BN": ("sbuf", [128, 1024], "bfloat16"), "SI": ("sbuf", [128, 64], "int32"),
+    "dg0": ("sbuf", [128, 1024], "bfloat16"), "dg1": ("sbuf", [128, 1024], "bfloat16"),
+    "dg2": ("sbuf", [128, 1024], "bfloat16"), "dg3": ("sbuf", [128, 1024], "bfloat16"),
+    "Ud": ("sbuf", [128, 16384], "bfloat16"), "ONE": ("sbuf", [128, 1024], "bfloat16"),
+    "CI": ("sbuf", [128, 64], "int32"), "S4": ("sbuf", [128, 64], "int32"), "S5": ("sbuf", [128, 64], "int32"),
+    "so4": ("sbuf", [128, 64], "uint16"), "su": ("sbuf", [128, 64], "uint16"),
+    "ID": ("sbuf", [128, 128], "bfloat16"), "BT": ("sbuf", [128, 128], "bfloat16"), "BLK": ("sbuf", [128, 128], "bfloat16"),
+    "NROW": ("sbuf", [128, 128], "bfloat16"), "KROW": ("sbuf", [128, 128], "bfloat16"), "KR2": ("sbuf", [128, 128], "bfloat16"),
+    "PI": ("sbuf", [128, 1], "int32"), "KI": ("sbuf", [128, 1], "int32"), "KC": ("sbuf", [128, 1], "float32"),
+    "O8": ("sbuf", [128, 128], "float32"), "B8T": ("sbuf", [128, 128], "float32"), "B8": ("sbuf", [128, 128], "float32"),
+    "G16": ("sbuf", [128, 8], "bfloat16"),
+    "CC": ("sbuf", [128, 64], "float32"), "W1": ("sbuf", [128, 128], "float32"), "W2": ("sbuf", [128, 128], "float32"),
+    "W3": ("sbuf", [128, 128], "float32"), "W4": ("sbuf", [128, 128], "float32"), "W5": ("sbuf", [128, 128], "float32"),
+    "WA": ("sbuf", [128, 128], "bfloat16"), "WA2": ("sbuf", [128, 128], "bfloat16"), "DK": ("sbuf", [128, 128], "bfloat16"),
+    "IM2": ("sbuf", [128, 128], "bfloat16"), "IP2": ("sbuf", [128, 128], "bfloat16"), "IM1": ("sbuf", [128, 128], "bfloat16"),
+    "I2K": ("sbuf", [128, 128], "bfloat16"), "NBK": ("sbuf", [128, 128], "bfloat16"), "M05": ("sbuf", [128, 128], "bfloat16"),
+    "O16": ("sbuf", [128, 128], "float32"), "RK": ("sbuf", [128, 128], "bfloat16"),
+    "RMX": ("sbuf", [128, 1024], "bfloat16"), "RMN": ("sbuf", [128, 1024], "bfloat16"), "M01": ("sbuf", [128, 1024], "bfloat16"),
+    "dgL": ("sbuf", [128, 1024], "bfloat16"), "IM16": ("sbuf", [128, 128], "bfloat16"),
+    "I64": ("sbuf", [128, 128], "bfloat16"), "IBG": ("sbuf", [128, 128], "bfloat16"), "RS": ("sbuf", [128, 128], "bfloat16"),
+    "IT1": ("sbuf", [128, 128], "bfloat16"), "IT2": ("sbuf", [128, 128], "bfloat16"), "IT3": ("sbuf", [128, 128], "bfloat16"),
+    "BS": ("sbuf", [128, 128], "bfloat16"), "BW": ("sbuf", [128, 128], "bfloat16"), "MAD": ("sbuf", [128, 128], "bfloat16"),
+    "V40": ("sbuf", [128, 128], "bfloat16"), "V41": ("sbuf", [128, 128], "bfloat16"),
+    "TH8": ("sbuf", [8, 4], "int32"), "THF": ("sbuf", [8, 4], "float32"), "THC": ("sbuf", [128, 4], "float32"),
+    "RI": ("sbuf", [128, 1], "int32"), "RA": ("sbuf", [128, 1], "int32"), "THR": ("sbuf", [128, 4], "float32"),
+    "CNT": ("sbuf", [128, 2], "float32"), "XN": ("sbuf", [128, 256], "bfloat16"),
+    "sI1": ("sbuf", [128, 512], "bfloat16"), "sI2": ("sbuf", [128, 512], "bfloat16"),
+}
+for _h in range(2):
+    for _n, _w, _d in (("WIN", WINW, "bfloat16"), ("EJ", 128, "uint16"), ("PC", 128, "bfloat16"), ("NO", 128, "bfloat16"),
+                       ("ZX", 1024, "bfloat16"), ("XE", 2048, "bfloat16"), ("D", 2048, "bfloat16"), ("AB", 2048, "bfloat16"),
+                       ("G", 2048, "bfloat16"), ("MX", 2048, "bfloat16"), ("MN", 2048, "bfloat16"), ("KM", 128, "float32"),
+                       ("ZK", 128, "float32"), ("KE", 128, "float32"), ("HIT", 128, "bfloat16"), ("E2", 128, "float32"),
+                       ("EO", 128, "uint16"), ("RT", 128, "float32"), ("F0", 128, "bfloat16"), ("Z0", 128, "bfloat16"),
+                       ("SLI", 8, "int32"), ("SLA", 8, "int32"), ("SLO", 8, "uint16"), ("DG", 128, "bfloat16"),
+                       ("WLO", 8, "uint16"), ("EG", 128, "float32"), ("BG", 128, "bfloat16"), ("XG", 128, "bfloat16"),
+                       ("DD1", 128, "bfloat16"), ("DD2", 128, "bfloat16"), ("AD", 128, "bfloat16"), ("ST", 128, "bfloat16"),
+                       ("SX", 128, "bfloat16"), ("SH", 128, "bfloat16"), ("MF", 2048, "bfloat16"), ("NF", 2048, "bfloat16"),
+                       ("LF", 128, "float32")):
+        SCRATCH["%s%d" % (_n, _h)] = ("sbuf", [128, _w], _d)
+    for _b in range(4):
+        SCRATCH["P%d%d" % (_b, _h)] = ("psum", [128, 512], "float32")
+for _t in range(3):
+    SCRATCH["la%d" % _t] = ("sbuf", [128, 256], "bfloat16")
+    SCRATCH["sa%d" % _t] = ("sbuf", [128, 128], "bfloat16")
+    SCRATCH["sb%d" % _t] = ("sbuf", [128, 128], "bfloat16")
+
+ALIAS = {}
+
+
+def together(big, names):
+    dtype = SCRATCH[names[0]][2]
+    for k, nm in enumerate(names):
+        ALIAS[nm] = (big, 128 * k)
+        del SCRATCH[nm]
+    SCRATCH[big] = ("sbuf", [128, 128 * len(names)], dtype)
+
+
+together("CB", ["ID", "BT", "BLK", "NROW", "KROW", "KR2", "WA", "WA2", "DK", "IM2", "IP2", "IM1", "I2K", "NBK", "M05", "RK", "IM16", "I64", "IBG",
+                "IT1", "IT2", "IT3", "BS", "BW", "MAD", "V40", "V41", "RS"])
+together("CF", ["W1", "W2", "W3", "W4", "W5"])
+for _h in range(2):
+    together("FH%d" % _h, [_n + str(_h) for _n in ("KM", "ZK", "KE", "E2", "EG", "RT", "LF")])
+    together("BH%d" % _h, [_n + str(_h) for _n in ("PC", "NO", "HIT", "F0", "Z0", "DD1", "DD2", "AD", "ST", "SX", "SH")])
+for _t in range(3):
+    together("ss%d" % _t, ["sa%d" % _t, "sb%d" % _t])
+
+
+def cols(T, name, a=0, b=None, s=1):
+    if name in ALIAS:
+        big, o = ALIAS[name]
+        b = 128 if b is None else b
+        return T[big][:, o + a:o + b:s] if s != 1 else T[big][:, o + a:o + b]
+    if b is None:
+        return T[name][:]
+    return T[name][:, a:b:s] if s != 1 else T[name][:, a:b]
+
+
+NDMA = 40
+SEMAPHORES = ["cv", "ca", "cp", "cg", "loc"] + ["arr%d" % _t for _t in range(4)] + ["dm%d" % _t for _t in range(NDMA)]
+
+CY = 1.0e-3 * 0.95
+GC = 1.5
+SLAT = 0.08
+PARAM_AFTER = []
+AHEAD = 3.0
+WINDOW, SLACK = 0.6, 0.3
+PRIO = {'vDD20': -2.1, 'aZ00': -2.2, 'vMX0.2': -1.3, 'vMN0.2': 6.4, 'vST1': 4.4, 'vEE.3': 3.6, 'aG0.3': -2.0, 'vZK1': 2.1, 'vSLO1': 1.8, 'aAB1.1.1': -11.5, 'aAD1': 3.6, 'asb1': 2.7, 'vMN1.2': -0.6, 'aBG0': 0.2, 'vMN1.1': 0.5, 'asb2': 0.6, 'aW1.g': 1.8, 'vRI': -2.2, 'vD1.0': -5.7, 'vDD10': -0.6, 'vNF1.0': 2.7, 'vXE1.1': -2.2, 'vEE.1': 4.5, 'vSLA1': 3.3, 'aW1.x0': -7.9, 'vMX0.0': 5.4, 'vW1': 0.5, 'vMX1.0': 0.3, 'vZK0': 0.6, 'vMF1.0': 2.0, 'vST0': 0.7, 'pP20': -5.9, 'aAB1.0.0': -4.8, 'aZ01': -0.8, 'aW1.z': 6.4, 'vE21': 4.0, 'aAB0.0.0': -1.0, 'aD0.1': -1.7, 'aAB1.1.0': 0.8, 'vHIT1': 0.1, 'pP10': 0.9, 'aPC1': -9.5, 'vsa2': 1.3, 'vMN0.1': -2.9, 'vRA': 1.0, 'aEG1': -1.3, 'vEG1': 3.8, 'aNO0': -0.4, 'aDG1': 2.2, 'vMX0.1': 0.9, 'vSLI0': 2.9, 'vMX0.3': -0.3, 'vD0.0': -2.6, 'vSX1': -0.1, 'vMX1.1': 0.1, 'vEJ1': 0.5, 'vW0.x0': -4.7, 'vKM0': 5.9, 'vXN.1': -1.8, 'vW0.x1': 2.7, 'vKE0': 2.8, 'aAD0': -9.2, 'vMF0.1': -0.6, 'aG1.3': -0.8, 'vLF0': -0.3, 'aDG0': 1.7, 'aPC0': 0.4, 'aRT0': 3.9, 'vTHR': 1.5, 'vHIT0': 0.3, 'vNF1.1': 0.3, 'vDG0': -0.9, 'vKE1': 1.9, 'vSLA0': 2.2, 'vEE.2': 0.1, 'aRT1': 2.6, 'vG1.0': 6.5, 'vDD11': -0.5}
+BCH = 512
+PARAM = {"judge": [[0, 1], [0, 1]], "bulk": [[[1, 1, 1, 1], [1, 1, 1, 1]], [[0, 1, 1, 1], [0, 1, 1, 1]], [[0, 1, 1, 1], [0, 1, 1, 1]]],
+         "dg": [[1, 1], [1, 1]], "eg": [[1, 1], [1, 0]]}
+
+
+def build():
+    ops = []
+    ndma = [0]
+    half = [1]
+    after = []
+
+    def op(q, fn, r, w, cost, n=1, lat=0.0, sem=None):
+        ops.append({"q": q, "fn": fn, "r": r, "w": w, "cost": cost, "n": n, "lat": lat, "sem": sem, "i": len(ops), "after": after[:],
+                    "h": half[0]})
+
+    def vec(fn, r, w, cyc):
+        op("v", fn, r, w, max(64, cyc) * CY + 0.02)
+
+    def act(fn, r, w, cyc):
+        op("a", fn, r, w, max(64, cyc) * CY + 0.02)
+
+    def pe(fn, r, w, cyc, n):
+        op("p", fn, r, w, cyc * CY, n)
+
+    def gp(fn, r, w, cyc):
+        op("g", fn, r, w, cyc * CY + 0.15)
+
+    def dma(q, fn, r, w, lat):
+        op(q, fn, r, w, 0.06, 1, lat, "dm%d" % ndma[0])
+        ndma[0] += 1
+
+    def vcopy(o, i):
+        return lambda g, T: g.vector.tensor_copy(o(T), i(T))
+
+    def vts(o, i, s1, o1, s2=None, o2=None):
+        def fn(g, T):
+            a = s1(T) if callable_(s1) else s1
+            if o2 is None:
+                return g.vector.tensor_scalar(o(T), i(T), a, None, o1)
+            b = s2(T) if callable_(s2) else s2
+            return g.vector.tensor_scalar(o(T), i(T), a, b, o1, o2)
+        return fn
+
+    def callable_(x):
+        return not isinstance(x, (int, float))
+
+    def vtt(o, a, b, f):
+        return lambda g, T: g.vector.tensor_tensor(o(T), a(T), b(T), f)
+
+    def aact(o, i, f, bias=0.0, scale=1.0):
+        return lambda g, T: g.scalar.activation(o(T), i(T), f, bias=bias, scale=scale)
+
+    def buf(name, a=None, b=None, s=1):
+        return lambda T: cols(T, name, a or 0, b, s)
+
+    def ind(name, a, b, off, c, d):
+        return lambda T: T[name][:, a:b].indirect(T[off][:, c:d])
+
+    def mms(lst):
+        def fn(g, T):
+            return [g.tensor.matmul(o(T), l(T), r(T), s, e) for o, l, r, s, e in lst]
+        return fn
+
+    def fill(name, val, a=None, b=None, s=1):
+        x = buf(name, a, b, s)
+        return lambda g, T: g.vector.memset(x(T), val)
+
+    WX = [["W%d.x%d" % (h, c) for c in range(4)] for h in range(2)]
+    WALL = [WX[h] + ["W%d.g" % h, "W%d.y" % h, "W%d.z" % h] for h in range(2)]
+
+    dma("s", lambda g, T: g.sync.dma_start(T.SI[:], T.snd[:]), [], ["SI"], 1.8)
+    dma("a", lambda g, T: g.scalar.dma_start(T.WIN0[:, 0:V], T.xa[:]), [], WX[0], 2.2)
+    dma("s", lambda g, T: g.sync.dma_start(T.EI[:], T.ent[:]), [], ["EI"], 3.0)
+    dma("a", lambda g, T: g.scalar.dma_start(T.UI[:], T.usr[:]), [], ["UI"], 3.6)
+    dma("s", lambda g, T: g.sync.dma_start(T.TH8[:], T.th[:]), [], ["TH8"], 3.0)
+    dma("s", lambda g, T: g.sync.dma_start(T.WIN0[:, 2048:4096], T.yc[:]), [], ["W0.y"], 4.5)
+    dma("a", lambda g, T: g.scalar.dma_start(T.WIN1[:, 0:V], T.xa[:]), [], WX[1], 4.5)
+    dma("s", lambda g, T: g.sync.dma_start(T.WIN1[:, 2048:4096], T.yc[:]), [], ["W1.y"], 5.5)
+    dma("a", lambda g, T: g.scalar.dma_start(T.BN[:], T.bn[:]), [], ["BN"], 5.5)
+
+    gp(lambda g, T: g.iota(T.CI[:], [[0, 2], [1, 4], [0, 8]], 0, 0), [], ["CI"], 128)
+    vec(vts(buf("S4"), buf("SI"), 4, A.mult), ["SI"], ["S4"], 64)
+    vec(vtt(buf("S5"), buf("S4"), buf("CI"), A.add), ["S4", "CI"], ["S5"], 128)
+    vec(vcopy(buf("so4"), buf("S5")), ["S5"], ["so4"], 64)
+    vec(lambda g, T: g.vector.tensor_copy(T.sI1[:], T.WIN0[:, 0:V].indirect(T.so4[:, 0:32])), ["so4"] + WX[0], ["sI1"], 60 + 512 * GC)
+    act(lambda g, T: g.scalar.activation(T.sI2[:], T.WIN0[:, 0:V].indirect(T.so4[:, 32:64]), F.Copy), ["so4"] + WX[0], ["sI2"], 75 + 512 * GC)
+    op("g", ("send", 0, "sI1", "sI2"), ["sI1", "sI2"], ["sent0"], 1.0)
+    op("x", None, ["sent0"], ["W0.g"], 0.0, 1, 5.0, "arr0")
+    vec(vcopy(buf("su"), buf("SI")), ["SI"], ["su"], 64)
+
+    vec(fill("ONE", 1.0), [], ["ONE"], 512)
+    gp(lambda g, T: g.affine_select(cols(T, "BT"), T.ONE[:, 0:128], [[-16, 8], [0, 16]], A.is_ge, 0.0, 0, 1), ["ONE"], ["BT"], 256)
+    gp(lambda g, T: g.affine_select(cols(T, "BLK"), cols(T, "BT"), [[16, 8], [0, 16]], A.is_ge, 0.0, 15, -1), ["BT"], ["BLK"], 256)
+    gp(lambda g, T: g.iota(T.PI[:], [[1, 1]], 0, 1), [], ["PI"], 2)
+    gp(lambda g, T: g.affine_select(cols(T, "ID"), T.ONE[:, 0:128], [[-1, 128]], A.is_equal, 0.0, 0, 1), ["ONE"], ["ID"], 256)
+    gp(lambda g, T: g.iota(cols(T, "NROW"), [[1, 128]], 0, 0, allow_small_or_imprecise_dtypes=True), [], ["NROW"], 256)
+    gp(lambda g, T: g.iota(cols(T, "KROW"), [[0, 8], [1, 16]], 0, 0, allow_small_or_imprecise_dtypes=True), [], ["KROW"], 256)
+    vec(fill("O8", 1.0), [], ["O8"], 128)
+    gp(lambda g, T: g.affine_select(T.B8T[0:8, :], T.O8[0:8, :], [[1, 128]], A.is_ge, 0.0, 0, -16), ["O8"], ["B8T"], 256)
+    gp(lambda g, T: g.affine_select(T.B8[0:8, :], T.B8T[0:8, :], [[-1, 128]], A.is_ge, 0.0, 15, 16), ["B8T"], ["B8"], 256)
+    vec(fill("RMX", 0.0), [], ["RMX"], 512)
+    vec(fill("RMX", -1024.0, 0, 1024, 16), [], ["RMX"], 64)
+    vec(fill("ZX0", 0.0), [], ["ZX0"], 512)
+    act(aact(buf("RMN"), buf("RMX"), F.Copy, 0.0, -1.0), ["RMX"], ["RMN"], 1024)
+    act(aact(buf("M01"), buf("RMX"), F.Identity, 1.0, 1.0 / 1024), ["RMX"], ["M01"], 1024)
+    vec(fill("ZX1", 0.0), [], ["ZX1"], 512)
+    vec(fill("RK", 0.0), [], ["RK"], 64)
+    vec(fill("RK", 2097152.0, 0, 128, 16), [], ["RK"], 64)
+    vec(fill("M05", -0.5), [], ["M05"], 64)
+    vec(fill("O16", 1.0 / 16), [], ["O16"], 128)
+    for h in range(2):
+        vec(fill("ZK%d" % h, 0.0), [], ["ZK%d" % h], 128)
+    vec(fill("RS", 0.0), [], ["RS"], 64)
+    vec(fill("RS", -16777216.0, 0, 128, 16), [], ["RS"], 64)
+    vec(vts(buf("KI"), buf("PI"), 15, A.bitwise_and), ["PI"], ["KI"], 64)
+    vec(vcopy(buf("KC"), buf("KI")), ["KI"], ["KC"], 64)
+    vec(vts(buf("G16"), buf("BLK", 0, 128, 16), 16.0, A.mult), ["BLK"], ["G16"], 64)
+    vec(vts(buf("CC", 0, 1), buf("KC"), 0.0, A.is_equal, 8.0, A.mult), ["KC"], ["CC0"], 64)
+    vec(vts(buf("CC", 8, 9), buf("KC"), 1.0, A.is_equal), ["KC"], ["CC1"], 64)
+    vec(vts(buf("CC", 18, 19), buf("KC"), 4.0, A.is_equal, -1168.0, A.mult), ["KC"], ["CC4"], 64)
+    vec(vtt(buf("CC", 19, 20), buf("CC", 0, 1), buf("CC", 8, 9), A.add), ["CC0", "CC1"], ["CC3"], 64)
+    vec(vtt(buf("CC", 16, 17), buf("CC", 18, 19), buf("CC", 19, 20), A.add), ["CC3", "CC4"], ["CC2"], 64)
+    vec(vts(buf("BW"), buf("BLK"), buf("CC", 16, 17), A.mult), ["BLK", "CC2"], ["BW"], 64)
+    vec(vts(buf("MAD"), buf("KROW"), buf("KC"), A.not_equal, -8388608.0, A.mult), ["KROW", "KC"], ["MAD"], 64)
+    for h in range(2):
+        act(aact(buf("V4%d" % h), buf("NROW"), F.Identity, 512.0 * h, 4.0), ["NROW"], ["V4%d" % h], 128)
+    for j, (k, val) in enumerate(((2, 16384.0), (3, -8192.0), (4, -8192.0), (5, 4096.0), (5, 2048.0))):
+        vec(vts(buf("CC", 24 + 8 * j, 25 + 8 * j), buf("KC"), float(k), A.is_equal, val, A.mult), ["KC"], ["CD%d" % j], 64)
+    vec(vtt(buf("KR2"), buf("KROW"), buf("KROW"), A.mult), ["KROW"], ["KR2"], 256)
+    vec(vts(buf("W1"), buf("KROW"), buf("CC", 24, 25), A.mult), ["KROW", "CD0"], ["W1"], 128)
+    vec(vts(buf("W2"), buf("KR2"), buf("CC", 40, 41), A.mult, buf("CC", 32, 33), A.add), ["KR2", "CD1", "CD2"], ["W2"], 128)
+    vec(vtt(buf("W3"), buf("W1"), buf("W2"), A.add), ["W1", "W2"], ["W3"], 256)
+    vec(vts(buf("W4"), buf("W3"), buf("CC", 48, 49), A.add), ["W3", "CD3"], ["W4"], 128)
+    vec(vts(buf("W5"), buf("W3"), -1.0, A.mult, buf("CC", 56, 57), A.add), ["W3", "CD4"], ["W5"], 128)
+    vec(vtt(buf("WA"), buf("W4"), buf("BLK"), A.mult), ["W4", "BLK"], ["WA"], 256)
+    vec(vtt(buf("WA2"), buf("W5"), buf("BLK"), A.mult), ["W5", "BLK"], ["WA2"], 256)
+    vec(vts(buf("DK"), buf("ID"), buf("KC"), A.mult), ["ID", "KC"], ["DK"], 128)
+    for nm, val, src in (("IM2", -2.0, "ID"), ("IP2", 2.0, "ID"), ("I64", 65536.0, "ID"), ("IBG", 1048576.0, "ID"), ("IM1", -1.0, "ID"), ("I2K", 2048.0, "ID"), ("IM16", -16.0, "ID"), ("IT1", 1.0, "ID"), ("IT2", 2.0, "ID"), ("IT3", 3.0, "ID"), ("BS", 1024.0, "BLK"), ("NBK", -8192.0, "BLK")):
+        act(aact(buf(nm), buf(src), F.Copy, 0.0, val), [src], [nm], 128)
+    vec(vcopy(buf("THF"), buf("TH8")), ["TH8"], ["THF"], 64)
+    pe(mms([(buf("P30", 0, 4), lambda T: T.B8[0:8, :], lambda T: T.THF[:], True, True)]), ["B8", "THF"], ["P30"], 256, 1)
+    vec(vcopy(buf("THC"), buf("P30", 0, 4)), ["P30"], ["THC"], 64)
+    vec(vcopy(buf("THR", 0, 1), buf("THC", 0, 1)), ["THC"], ["THR"], 64)
+
+    vec(vts(buf("dg0"), buf("UI"), 1.0 / 128, A.mult, 129.0 - 127.0 / 256, A.add), ["UI"], ["dg0"], 1024)
+    vec(vts(buf("UT"), buf("UI"), 127, A.bitwise_and), ["UI"], ["UT"], 1024)
+    vec(vcopy(buf("dgL"), buf("UT")), ["UT"], ["dgL"], 1024)
+    vec(vts(buf("dg1"), buf("dgL"), 1.0 / 16, A.mult, 136.0 - 15.0 / 32, A.add), ["dgL"], ["dg1"], 512)
+    for b in range(2):
+        p = "P0%d" % b
+        pe(mms([(buf(p), buf("ID"), buf("dgL", 512 * b, 512 * b + 512), True, False),
+                (buf(p), buf("IM16"), buf("dg1", 512 * b, 512 * b + 512), False, True)]), ["ID", "IM16", "dgL", "dg1"], [p], 1024, 2)
+        act(aact(buf("dg2", 512 * b, 512 * b + 512), buf(p), F.Identity, 2176.0), [p], ["dg2"], 512)
+    act(aact(buf("dg3"), buf("dg2"), F.Square), ["dg2"], ["dg3"], 1024)
+
+    def flat(d, src):
+        return lambda g, T: g.sync.dma_start(T.Ud[d::16, :], T[src][:])
+    for d in range(4, 16):
+        dma("s", flat(d, "ONE"), ["ONE", "sent0"], ["Ud.%d" % d], 2.0 + 0.7 * (d - 3))
+    for d in range(4):
+        dma("s", flat(d, "dg%d" % d), ["dg%d" % d], ["Ud.%d" % d], 3.0)
+    UDK = ["Ud.%d" % d for d in range(16)]
+    EEK = ["EE.%d" % c for c in range(4)]
+    vec(vcopy(buf("EE"), buf("EI")), ["EI"], EEK, 1024)
+
+    def cls(t, h):
+        return t + 512 * h, 512 * h + 512, 4
+
+    def prep(t):
+        for h in range(2):
+            a, b, s = cls(t, h)
+            H = "%d" % h
+            for c in range(2):
+                vec(vcopy(buf("ZX" + H, 0, 1024, 16), buf("WIN0", a + 256 * c, 512 * h + 256 * c + 256, s)), ["W0.x%d" % t, "ZX" + H], ["ZX" + H], 64)
+                vec(lambda g, T, H=H, c=c: g.vector.tensor_tensor_scan(T["XE" + H][:, 1024 * c:1024 * c + 1024], T.M01[:], T["ZX" + H][:], 0.0, A.mult, A.add),
+                    ["M01", "ZX" + H], ["XE%s.%d" % (H, c)], 512)
+            vec(vcopy(buf("EJ" + H), buf("EI", a, b, s)), ["EI"], ["EJ" + H], 128)
+            act(aact(buf("PC" + H), buf("EE", a, b, s), F.Sign, -2047.5), ["EE.%d" % t], ["PC" + H], 128)
+            pe(mms([(buf("P0" + H, 128, 256), buf("BLK"), buf("PC" + H), True, True)]), ["BLK", "PC" + H], ["P0" + H], 128, 1)
+            act(aact(buf("NO" + H), buf("P0" + H, 128, 256), F.Relu, -15.0), ["P0" + H], ["NO" + H], 128)
+
+    prep(0)
+    act(lambda g, T: g.scalar.activation(T.WIN1[:, 1024:2048], T.WIN0[:, 1024:2048], F.Copy), ["W0.g"], ["W1.g"], 1024)
+    for h in range(2):
+        vec(fill("WIN%d" % h, 0.0, 4096, 4224), [], ["W%d.z" % h], 64)
+
+    def rounding(h, bank, out, outkey):
+        H = "%d" % h
+        act(aact(buf("RT" + H), buf(bank, 0, 128), F.Identity, MAGIC, 0.5), [bank], ["RT" + H], 128)
+        act(aact(out, buf("RT" + H), F.Abs, -MAGIC, 1.0), ["RT" + H], [outkey], 128)
+
+    def scans(h, src, c, n, mx="MX", mn="MN"):
+        H = "%d" % h
+        a, b = n * c, n * c + n
+        for dst, res, f in ((mx + H, "RMX", A.max), (mn + H, "RMN", A.min)):
+            vec(lambda g, T, dst=dst, res=res, f=f: g.vector.tensor_tensor_scan(T[dst][:, a:b], T[res][:, 0:n], T[src][:, a:b], 0.0, A.add, f),
+                [res, "%s.%d" % (src, c)], ["%s.%d" % (dst, c)], n // 2)
+
+    def small(where, fout, fsrc, r, w):
+        if where:
+            act(lambda g, T: g.scalar.activation(fout(T), fsrc(T), F.Copy), r, w, 75 + 128 * GC)
+        else:
+            vec(lambda g, T: g.vector.tensor_copy(fout(T), fsrc(T)), r, w, 60 + 128 * GC)
+
+    def fmm(h, bank, bsrc, bkey, extra=(), mx="MX", mn="MN"):
+        H = "%d" % h
+        st = [(buf(bank, 0, 128), buf("ID"), buf("M05"), True, False), (buf(bank, 0, 128), buf("IM2"), bsrc, False, False)]
+        rk = ["ID", "M05", "IM2", bkey]
+        for c, src, key in extra:
+            st.append((buf(bank, 64 * c, 64 * c + 64), buf("IP2"), src, False, False))
+            rk += ["IP2", key]
+        pe(mms(st), rk, [bank], 128 * len(st), len(st))
+        ks = ["%s%d.%d" % (m, h, c) for m in (mx, mn) for c in range(2 if mx == "MF" else 2048 // BCH)]
+        pe(mms([(buf(bank, 0, 128), buf("ID"), buf(mx + H, 15, 2048, 16), False, False),
+                (buf(bank, 0, 128), buf("ID"), buf(mn + H, 15, 2048, 16), False, True)]), ["ID"] + ks, [bank], 256, 2)
+
+    def bulk(h, hop):
+        H = "%d" % h
+        for c in range(2048 // BCH):
+            src = ind("WIN" + H, 0, WINW, "EO" + H, BCH // 16 * c, BCH // 16 * (c + 1))
+            out = buf("G" + H, BCH * c, BCH * c + BCH)
+            if PARAM["bulk"][hop][h][c]:
+                act(lambda g, T, o=out, s=src: g.scalar.activation(o(T), s(T), F.Copy), WALL[h] + ["EO" + H], ["G%d.%d" % (h, c)], 75 + BCH * GC)
+            else:
+                vec(lambda g, T, o=out, s=src: g.vector.tensor_copy(o(T), s(T)), WALL[h] + ["EO" + H], ["G%d.%d" % (h, c)], 60 + BCH * GC)
+        for c in range(2048 // BCH):
+            scans(h, "G" + H, c, BCH)
+
+    def diagonal(h, bank):
+        H = "%d" % h
+        vec(lambda g, T: g.vector.tensor_tensor_scan(cols(T, "LF" + H), cols(T, "RS"), T[bank][:, 0:128], 0.0, A.add, A.max),
+            ["RS", bank], ["LF" + H], 128)
+
+    for t in range(RO):
+        for h in range(2):
+            half[0] = h
+            H = "%d" % h
+            a, b, s = cls(t, h)
+            for c in range(2):
+                p, q = 1024 * c, 1024 * c + 1024
+                src = ind("WIN" + H, 0, WINW, "EJ" + H, 64 * c, 64 * c + 64)
+                rk, dk, ak = WALL[h] + ["EJ" + H], "D%d.%d" % (h, c), "AB%d.%d" % (h, c)
+                if PARAM["judge"][h][c]:
+                    act(lambda g, T, o=buf("D" + H, p, q), s=src: g.scalar.activation(o(T), s(T), F.Copy), rk, [dk], 75 + 1024 * GC)
+                    for j in range(2):
+                        u, w, pb = p + 512 * j, p + 512 * j + 512, "P%d%s" % (3 - 2 * j, H)
+                        pe(mms([(buf(pb), buf("IM1"), buf("XE" + H, u, w), True, False), (buf(pb), buf("ID"), buf("D" + H, u, w), False, True)]),
+                           ["IM1", "ID", dk, "XE%s.%d" % (H, c)], [pb], 1024, 2)
+                        act(aact(buf("AB" + H, u, w), buf(pb), F.Abs), [pb], ["%s.%d" % (ak, j)], 512)
+                else:
+                    vec(lambda g, T, o=buf("D" + H, p, q), s=src, x=buf("XE" + H, p, q): g.vector.tensor_tensor(o(T), s(T), x(T), A.subtract),
+                        rk + ["XE%s.%d" % (H, c)], [dk], 60 + 1024 * GC)
+                    act(aact(buf("AB" + H, p, q), buf("D" + H, p, q), F.Abs), [dk], [ak + ".0", ak + ".1"], 1024)
+            pe(mms([(buf("P0" + H, 0, 128), buf("PC" + H), buf("I64"), True, False),
+                    (buf("P0" + H, 0, 128), buf("ONE", 0, 128), buf("DK"), False, False)]), ["PC" + H, "I64", "ONE", "DK"], ["P0" + H], 256, 2)
+            pe(mms([(buf("P0" + H, k, 128, 16), buf("AB" + H, k, 2048, 16), buf("G16"), False, k == 15) for k in range(16)]),
+               ["AB%d.%d.%d" % (h, c, j) for c in range(2) for j in range(2)] + ["G16"], ["P0" + H], 1024, 16)
+            vec(lambda g, T, H=H: g.vector.tensor_tensor_scan(cols(T, "KM" + H), cols(T, "RK"), T["P0" + H][:, 0:128], 0.0, A.add, A.min),
+                ["RK", "P0" + H], ["KM" + H], 128)
+            vec(vcopy(buf("ZK" + H, 0, 128, 16), buf("KM" + H, 15, 128, 16)), ["KM" + H, "ZK" + H], ["ZK" + H], 64)
+            vec(lambda g, T, H=H: g.vector.tensor_tensor_scan(cols(T, "KE" + H), T.M01[:, 0:128], cols(T, "ZK" + H), 0.0, A.mult, A.add),
+                ["M01", "ZK" + H], ["KE" + H], 128)
+            vec(vtt(buf("HIT" + H), buf("P0" + H, 0, 128), buf("KE" + H), A.is_equal), ["P0" + H, "KE" + H], ["HIT" + H], 128)
+            pe(mms([(buf("P1" + H, 0, 128), buf("HIT" + H), buf("I2K"), True, True)]), ["HIT" + H, "I2K"], ["P1" + H], 128, 1)
+            vec(vtt(buf("E2" + H), buf("EI", a, b, s), buf("P1" + H, 0, 128), A.add), ["EI", "P1" + H], ["E2" + H], 128)
+            vec(vts(buf("EO" + H), buf("E2" + H), 4095.0, A.min), ["E2" + H], ["EO" + H], 128)
+            xv = [(c, buf("WIN" + H, a + 256 * c, 256 * c + 512 * h + 256, s), "W%d.x%d" % (h, t)) for c in range(2) if not PARAM["judge"][h][c]]
+            for c in range(2):
+                scans(h, "D" + H, c, 1024, "MF", "NF")
+            fmm(h, "P2" + H, buf("BN", a, b, s), "BN", xv, "MF", "NF")
+            rounding(h, "P2" + H, buf("F0" + H), "F0" + H)
+            bulk(h, 0)
+            fmm(h, "P3" + H, buf("BN", a, b, s), "BN")
+            rounding(h, "P3" + H, buf("WIN" + H, 4096, 4224), "W%d.z" % h)
+            act(aact(buf("Z0" + H), buf("RT" + H), F.Abs, -MAGIC, 1.0), ["RT" + H], ["Z0" + H], 128)
+            for hop in (1, 2):
+                p0 = buf("P0" + H, 0, 128)
+                st, rk = [(p0, buf("ID"), buf("MAD"), True, False)], ["ID", "MAD"]
+                if hop == 1:
+                    st.append((p0, buf("ID"), buf("V4%d" % h), False, False))
+                    rk.append("V4%d" % h)
+                    if t:
+                        st.append((p0, buf("IT%d" % t), buf("ONE", 0, 128), False, False))
+                        rk += ["IT%d" % t, "ONE"]
+                else:
+                    st.append((p0, buf("BW"), buf("DG" + H), False, False))
+                    rk += ["BW", "DG" + H]
+                pe(mms(st), rk, ["P0" + H], 128 * len(st), len(st))
+                pe(mms([(p0, buf("BS"), buf("WIN" + H, 4096, 4224), False, True)]), ["BS", "W%d.z" % h], ["P0" + H], 128, 1)
+                diagonal(h, "P0" + H)
+                vec(vcopy(buf("SLI" + H), buf("LF" + H, 15, 128, 16)), ["LF" + H], ["SLI" + H], 64)
+                vec(vts(buf("SLA" + H), buf("SLI" + H), 16383, A.bitwise_and), ["SLI" + H], ["SLA" + H], 64)
+                vec(vcopy(buf("SLO" + H), buf("SLA" + H)), ["SLA" + H], ["SLO" + H], 64)
+                small(PARAM["dg"][hop - 1][h], buf("DG" + H), ind("Ud", 0, 16384, "SLO" + H, 0, 8), UDK + ["SLO" + H], ["DG" + H])
+                pe(mms([(buf("P1" + H, 0, 128), buf("ID"), buf("MAD"), True, False)]), ["ID", "MAD"], ["P1" + H], 128, 1)
+                pe(mms([(buf("P1" + H, 0, 128), buf("BW"), buf("DG" + H), False, True)]), ["BW", "DG" + H], ["P1" + H], 128, 1)
+                pe(mms([(buf("P2" + H, 0, 128), buf("ID"), buf("NROW"), True, False), (buf("P2" + H, 0, 128), buf("WA"), buf("DG" + H), False, True),
+                        (buf("P2" + H, 128, 256), buf("WA2"), buf("DG" + H), True, True)]), ["ID", "NROW", "WA", "WA2", "DG" + H], ["P2" + H], 384, 3)
+                diagonal(h, "P1" + H)
+                vec(vcopy(buf("WLO" + H), buf("LF" + H, 15, 128, 16)), ["LF" + H], ["WLO" + H], 64)
+                small(PARAM["eg"][hop - 1][h], buf("EG" + H), ind("EE", 0, 1024, "WLO" + H, 0, 8), EEK + ["WLO" + H], ["EG" + H])
+                vec(vtt(buf("E2" + H), buf("EG" + H), buf("P2" + H, 0, 128), A.max), ["EG" + H, "P2" + H], ["E2" + H], 128)
+                vec(vcopy(buf("EO" + H), buf("E2" + H)), ["E2" + H], ["EO" + H], 128)
+                act(lambda g, T, H=H: g.scalar.activation(T["BG" + H][:], T.BN[:, 0:1024].indirect(T["WLO" + H][:, 0:8]), F.Copy),
+                    ["BN", "WLO" + H], ["BG" + H], 75 + 128 * GC)
+                if hop == 2:
+                    act(lambda g, T, H=H: g.scalar.activation(T["XG" + H][:], T["WIN" + H][:, 0:1024].indirect(T["WLO" + H][:, 0:8]), F.Copy),
+                        WX[h] + ["WLO" + H], ["XG" + H], 75 + 128 * GC)
+                vec(vtt(buf("DD%d%d" % (hop, h)), buf("EG" + H), buf("P2" + H, 128, 256), A.is_ge), ["EG" + H, "P2" + H], ["DD%d%d" % (hop, h)], 128)
+                bulk(h, hop)
+                fmm(h, "P3" + H, buf("BG" + H), "BG" + H)
+                rounding(h, "P3" + H, buf("WIN" + H, 4096, 4224), "W%d.z" % h)
+            pe(mms([(buf("P3" + H, 0, 128), buf("IM1"), buf("XG" + H), True, False)]), ["IM1", "XG" + H], ["P3" + H], 128, 1)
+            pe(mms([(buf("P3" + H, 0, 128), buf("ID"), buf("WIN" + H, 4096, 4224), False, True)]), ["ID", "W%d.z" % h], ["P3" + H], 128, 1)
+            act(aact(buf("AD" + H), buf("P3" + H, 0, 128), F.Abs), ["P3" + H], ["AD" + H], 128)
+            pe(mms([(buf("P2" + H, 0, 128), buf("ID"), buf("Z0" + H), True, False), (buf("P2" + H, 0, 128), buf("IM1"), buf("F0" + H), False, True),
+                    (buf("P2" + H, 128, 256), buf("HIT" + H), buf("I2K"), True, True)]),
+               ["ID", "IM1", "I2K", "Z0" + H, "F0" + H, "HIT" + H], ["P2" + H], 384, 3)
+            pe(mms([(buf("P1" + H, 0, 128), buf("IBG"), buf("NO" + H), True, False), (buf("P1" + H, 0, 128), buf("NBK"), buf("DD1" + H), False, False),
+                    (buf("P1" + H, 0, 128), buf("NBK"), buf("DD2" + H), False, False)]), ["IBG", "NO" + H, "NBK", "DD1" + H, "DD2" + H], ["P1" + H], 384, 3)
+            pe(mms([(buf("P1" + H, 0, 128), buf("BLK"), buf("AD" + H), False, True)]), ["BLK", "AD" + H], ["P1" + H], 128, 1)
+            vec(vts(buf("ST" + H), buf("P1" + H, 0, 128), buf("THR", t, t + 1), A.is_le), ["P1" + H, "THR"], ["ST" + H], 128)
+            vec(vtt(buf("SX" + H), buf("ST" + H), buf("P2" + H, 0, 128), A.mult), ["ST" + H, "P2" + H], ["SX" + H], 128)
+            vec(vtt(buf("XN", 128 * h, 128 * h + 128), buf("F0" + H), buf("SX" + H), A.add), ["F0" + H, "SX" + H], ["XN.%d" % h], 256)
+        half[0] = 1
+        XNK = ["XN.0", "XN.1"]
+        if t < RO - 1:
+            vec(lambda g, T, t=t: g.vector.tensor_copy(cols(T, "sa%d" % t), T.XN[:, 0:256].indirect(T.su[:, 8 * t:8 * t + 8])), XNK + ["su"], ["sa%d" % t], 60 + 128 * GC)
+            act(lambda g, T, t=t: g.scalar.activation(cols(T, "sb%d" % t), T.XN[:, 0:256].indirect(T.su[:, 8 * t + 32:8 * t + 40]), F.Copy), XNK + ["su"], ["sb%d" % t], 75 + 128 * GC)
+            op("g", ("send", t + 1, "sa%d" % t, "sb%d" % t), ["sa%d" % t, "sb%d" % t], ["sent%d" % (t + 1)], 0.6)
+            op("x", None, ["sent%d" % (t + 1)], ["la%d" % t], 0.0, 1, 2.5, "arr%d" % (t + 1))
+            act(aact(buf("WIN1", t, 1024, 4), buf("XN"), F.Copy), XNK, ["W1.x%d" % t], 256)
+        vec(vcopy(buf("WIN0", t, 1024, 4), buf("XN")), XNK, ["W0.x%d" % t], 128)
+        if t == RO - 1:
+            dma("s", lambda g, T: g.sync.dma_start(T.yx[:], T.WIN0[:, 0:V]), WX[0], [], 2.0)
+        for h in range(2):
+            H = "%d" % h
+            a, b, s = cls(t, h)
+            vec(vtt(buf("SH" + H), buf("ST" + H), buf("P2" + H, 128, 256), A.mult), ["ST" + H, "P2" + H], ["SH" + H], 128)
+            pe(mms([(buf("P3" + H, 0, 128), buf("ID"), buf("SH" + H), True, True)]), ["ID", "SH" + H], ["P3" + H], 128, 1)
+            vec(vtt(buf("EE", a, b, s), buf("EI", a, b, s), buf("P3" + H, 0, 128), A.add), ["EI", "P3" + H], ["EE.%d" % t], 128)
+        if t == RO - 1:
+            dma("a", lambda g, T: g.scalar.dma_start(T.ye[:], T.EE[:]), EEK, [], 2.0)
+        else:
+            for h in range(2):
+                H = "%d" % h
+                act(lambda g, T, H=H, h=h: g.scalar.activation(cols(T, "AD" + H), cols(T, "ST" + H), F.Copy, accum_out=T.CNT[:, h:h + 1]),
+                    ["ST" + H], ["CNT", "AD" + H], 150)
+            pe(mms([(buf("P30", 0, 2), buf("O16"), buf("CNT"), True, True)]), ["O16", "CNT"], ["P30"], 256, 1)
+            vec(vcopy(buf("W1", 0, 2), buf("P30", 0, 2)), ["P30"], ["W1"], 64)
+            vec(vtt(buf("RI"), buf("W1", 0, 1), buf("W1", 1, 2), A.add), ["W1"], ["RI"], 64)
+            vec(vts(buf("RA"), buf("RI"), 31, A.bitwise_and), ["RI"], ["RA"], 64)
+            vec(vtt(buf("THR", t + 1, t + 2), buf("THC", t + 1, t + 2), buf("RA"), A.add), ["THC", "RA"], ["THR"], 64)
+            after.extend(PARAM_AFTER)
+            prep(t + 1)
+            del after[:]
+            for h in range(2):
+                for n in range(2):
+                    a = 1024 + 512 * n + 128 * t
+                    o, i = buf("WIN%d" % h, a, a + 128), buf("la%d" % t, 128 * n, 128 * n + 128)
+                    if h:
+                        act(aact(o, i, F.Copy), ["la%d" % t], ["W1.g"], 128)
+                    else:
+                        vec(vcopy(o, i), ["la%d" % t], ["W0.g"], 64)
+    return ops
+
+
+SEMQ = {"v": "cv", "a": "ca", "p": "cp", "g": "cg"}
+
+
+def is_psum(k):
+    return len(k) == 3 and k[0] == "P" and k[1] in "0123" and k[2] in "01"
+
+
+def link(ops):
+    lw, rd = {}, {}
+    pred = []
+    for o in ops:
+        p = {}
+        i = o["i"]
+
+        def add(j, wait):
+            p[j] = p.get(j, False) or wait
+        for k in o["after"]:
+            if k in lw:
+                add(lw[k], False)
+        for k in o["r"]:
+            if k in lw:
+                add(lw[k], True)
+            if is_psum(k):
+                for j in rd.get(k, []):
+                    if ops[j]["q"] != o["q"]:
+                        add(j, True)
+        for k in o["w"]:
+            if k in lw:
+                j = lw[k]
+                add(j, not (o["q"] == "p" and ops[j]["q"] == "p"))
+            for j in rd.get(k, []):
+                add(j, not (o["q"] == "p" and ops[j]["q"] == "p"))
+        for k in o["r"]:
+            rd.setdefault(k, []).append(i)
+        for k in o["w"]:
+            lw[k] = i
+            rd[k] = []
+        p.pop(i, None)
+        pred.append(p)
+    return pred
+
+
+def schedule(ops, pred):
+    n = len(ops)
+    succ = [[] for _ in range(n)]
+    for i in range(n):
+        for j in pred[i]:
+            succ[j].append(i)
+    LAT = SLAT
+    prio = [0.0] * n
+    for i in range(n - 1, -1, -1):
+        o = ops[i]
+        prio[i] = o["cost"] + o["lat"] + max([prio[k] + LAT for k in succ[i]], default=0.0)
+    for i in range(n):
+        o = ops[i]
+        if o["h"] == 0:
+            prio[i] += AHEAD
+        if o["w"]:
+            prio[i] += PRIO.get(o["q"] + o["w"][0], 0.0)
+    left = [len(pred[i]) for i in range(n)]
+    ready = {}
+    at = [0.0] * n
+    free = {}
+    order, fin = [], [0.0] * n
+    for i in range(n):
+        if left[i] == 0:
+            ready.setdefault(ops[i]["q"], []).append(i)
+    start = [0.0] * n
+    while len(order) < n:
+        best = None
+        for q, lst in ready.items():
+            if not lst:
+                continue
+            f = free.get(q, 0.0)
+            s = max(f, min(at[i] for i in lst))
+            j = max((i for i in lst if at[i] <= s + WINDOW), key=lambda i: (prio[i], -i))
+            if at[j] > s + 1e-9:
+                fit = [i for i in lst if at[i] <= s + 1e-9 and s + ops[i]["cost"] <= at[j] + SLACK * ops[i]["cost"]]
+                if fit:
+                    i = max(fit, key=lambda i: (prio[i], -i))
+                else:
+                    i, s = j, at[j]
+            else:
+                i = j
+            if best is None or s < best[0]:
+                best = (s, q, i)
+        s, q, i = best
+        ready[q].remove(i)
+        o = ops[i]
+        start[i] = s
+        free[q] = s + (o["cost"] if q != "x" else 0.0)
+        fin[i] = s + o["cost"] + o["lat"]
+        order.append(i)
+        for k in succ[i]:
+            wt = pred[k][i]
+            at[k] = max(at[k], fin[i] + (LAT if wt else 0.0))
+            left[k] -= 1
+            if left[k] == 0:
+                ready.setdefault(ops[k]["q"], []).append(k)
+    return order, start, fin
+
+
+CACHE = {}
+
+
+def plan():
+    if "p" not in CACHE:
+        ops = build()
+        pred = link(ops)
+        order, start, fin = schedule(ops, pred)
+        place = {i: k for k, i in enumerate(order)}
+        pos = {}
+        tot = {}
+        know = {}
+        seen = {}
+        prog = []
+        for i in order:
+            o = ops[i]
+            q = o["q"]
+            kn = dict(seen.get(q, {}))
+            waits = []
+            need = {}
+            for j, wt in pred[i].items():
+                if not wt:
+                    continue
+                sem, val = pos[j]
+                if sem is not None and val > need.get(sem, 0):
+                    need[sem] = val
+            for j in sorted(pred[i], key=lambda j: -place[j]):
+                if not pred[i][j]:
+                    continue
+                sem, val = pos[j]
+                if sem is None or kn.get(sem, 0) >= val:
+                    continue
+                waits.append((sem, need[sem]))
+                kn[sem] = max(kn.get(sem, 0), need[sem])
+                for s2, v2 in know[j].items():
+                    kn[s2] = max(kn.get(s2, 0), v2)
+            seen[q] = kn
+            kj = dict(kn)
+            if o["sem"] is not None:
+                pos[i] = (o["sem"], -1 if q == "x" else 16)
+                kj[o["sem"]] = 16 if q != "x" else 1
+                if q == "x":
+                    pos[i] = (o["sem"], 1)
+            elif isinstance(o["fn"], tuple):
+                pos[i] = (None, 0)
+            else:
+                sm = SEMQ[q]
+                tot[sm] = tot.get(sm, 0) + o["n"]
+                pos[i] = (sm, tot[sm])
+                kj[sm] = tot[sm]
+            know[i] = kj
+            prog.append((o, waits))
+        CACHE["p"] = (prog, tot, ops, order, start, fin)
+    return CACHE["p"]
+
+
+def engines_of(core, d1, d2, topo):
+    e1, e2 = topo.engines(core, d1), topo.engines(core, d2)
+    both = [e for e in e1 if e in e2]
+    only1, only2 = [e for e in e1 if e not in e2], [e for e in e2 if e not in e1]
+    if only1:
+        return only1, e2
+    if only2:
+        return e1, only2
+    return both[:len(both) // 2], both[len(both) // 2:]
+
+
+def bits(es):
+    return sum(1 << e for e in es)
+
+
+def rank_program(g, core, T, topo):
+    rank = T.rank_of(core)
+    if rank is None:
+        return
+    prog, tot, ops, order, start, fin = plan()
+    n = len(T.cores)
+    dst = [T.cores[(rank - k) % n] for k in (1, 2)]
+    for d in dst:
+        assert topo.may_write(core, d)
+    masks = engines_of(core, dst[0], dst[1], topo)
+    arrive = 0
+    for k in (1, 2):
+        c = T.cores[(rank + k) % n]
+        m = engines_of(c, T.cores[(rank + k - 1) % n], T.cores[(rank + k - 2) % n], topo)
+        arrive += len(m[k - 1])
+    queue = {"v": g.vector, "a": g.scalar, "p": g.tensor, "g": g, "s": g.sync}
+    sent = 0
+    arrs = {"arr%d" % k: arrive for k in range(4)}
+    for o, waits in prog:
+        q = o["q"]
+        if q == "x":
+            continue
+        for sem, val in waits:
+            queue[q].wait_ge(T.sem[sem], arrs.get(sem, val))
+        fn = o["fn"]
+        if isinstance(fn, tuple):
+            x = fn[1]
+            tr = []
+            for k in range(2):
+                rid, pid, _ = topo.addr(dst[k])
+                if x == 0:
+                    land = T.WIN0[:, 1024 + 512 * k:1536 + 512 * k]
+                else:
+                    land = T["la%d" % (x - 1)][:, 128 * k:128 * k + 128]
+                tr.append(RemoteDMATransfer(dst_ids=[DstId(rid=rid, pnc=pid)], dma_engine_mask=bits(masks[k]),
+                                            remote_sem=T.sem["arr%d" % x], src=cols(T, fn[2 + k]), dst=land))
+            g.remote_dma_fused(tr, local_sem=T.sem.loc)
+            sent += len(masks[0]) + len(masks[1])
+            continue
+        r = fn(g, T)
+        if o["sem"] is not None:
+            r.then_inc(T.sem[o["sem"]], 16)
+        elif isinstance(r, list):
+            for x in r:
+                x.then_inc(T.sem[SEMQ[q]], 1)
+        else:
+            r.then_inc(T.sem[SEMQ[q]], 1)
+    for sem, val in tot.items():
+        g.wait_ge(T.sem[sem], val)
+    for o in ops:
+        if o["sem"] is not None:
+            g.wait_ge(T.sem[o["sem"]], arrs.get(o["sem"], 16))
+    g.wait_ge(T.sem.loc, sent)

@@ -22,12 +22,13 @@ SCRATCH = {
     "CC": ("sbuf", [128, 64], "float32"), "W1": ("sbuf", [128, 128], "float32"), "W2": ("sbuf", [128, 128], "float32"),
     "W3": ("sbuf", [128, 128], "float32"), "W4": ("sbuf", [128, 128], "float32"), "W5": ("sbuf", [128, 128], "float32"),
     "WA": ("sbuf", [128, 128], "bfloat16"), "WA2": ("sbuf", [128, 128], "bfloat16"), "DK": ("sbuf", [128, 128], "bfloat16"),
-    "IM2": ("sbuf", [128, 128], "bfloat16"), "IP2": ("sbuf", [128, 128], "bfloat16"), "IM1": ("sbuf", [128, 128], "bfloat16"),
-    "I2K": ("sbuf", [128, 128], "bfloat16"), "NBK": ("sbuf", [128, 128], "bfloat16"), "M05": ("sbuf", [128, 128], "bfloat16"),
+    "IH": ("sbuf", [128, 128], "bfloat16"), "MGC": ("sbuf", [128, 128], "bfloat16"), "IM1": ("sbuf", [128, 128], "bfloat16"),
+    "I2K": ("sbuf", [128, 128], "bfloat16"), "NBK": ("sbuf", [128, 128], "bfloat16"), "M25": ("sbuf", [128, 128], "bfloat16"),
     "O16": ("sbuf", [128, 128], "float32"), "RK": ("sbuf", [128, 128], "bfloat16"),
-    "RMX": ("sbuf", [128, 1024], "bfloat16"), "RMN": ("sbuf", [128, 1024], "bfloat16"), "M01": ("sbuf", [128, 1024], "bfloat16"),
+    "RMX": ("sbuf", [128, 512], "bfloat16"), "RMN": ("sbuf", [128, 512], "bfloat16"),
     "dgL": ("sbuf", [128, 1024], "bfloat16"), "IM16": ("sbuf", [128, 128], "bfloat16"),
-    "I64": ("sbuf", [128, 128], "bfloat16"), "IBG": ("sbuf", [128, 128], "bfloat16"), "RS": ("sbuf", [128, 128], "bfloat16"),
+    "I64": ("sbuf", [128, 128], "bfloat16"), "IBG": ("sbuf", [128, 128], "bfloat16"), "RS": ("sbuf", [128, 256], "bfloat16"), "DG8": ("sbuf", [128, 128], "bfloat16"), "PF": ("sbuf", [128, 1], "float32"),
+
     "IT1": ("sbuf", [128, 128], "bfloat16"), "IT2": ("sbuf", [128, 128], "bfloat16"), "IT3": ("sbuf", [128, 128], "bfloat16"),
     "BS": ("sbuf", [128, 128], "bfloat16"), "BW": ("sbuf", [128, 128], "bfloat16"), "MAD": ("sbuf", [128, 128], "bfloat16"),
     "V40": ("sbuf", [128, 128], "bfloat16"), "V41": ("sbuf", [128, 128], "bfloat16"),
@@ -37,13 +38,13 @@ SCRATCH = {
     "sI1": ("sbuf", [128, 512], "bfloat16"), "sI2": ("sbuf", [128, 512], "bfloat16"),
 }
 for _h in range(2):
-    for _n, _w, _d in (("WIN", WINW, "bfloat16"), ("EJ", 128, "uint16"), ("PC", 128, "bfloat16"), ("NO", 128, "bfloat16"),
-                       ("ZX", 1024, "bfloat16"), ("XE", 2048, "bfloat16"), ("D", 2048, "bfloat16"), ("AB", 2048, "bfloat16"),
-                       ("G", 2048, "bfloat16"), ("MX", 2048, "bfloat16"), ("MN", 2048, "bfloat16"), ("KM", 128, "float32"),
-                       ("ZK", 128, "float32"), ("KE", 128, "float32"), ("HIT", 128, "bfloat16"), ("E2", 128, "float32"),
-                       ("EO", 128, "uint16"), ("RT", 128, "float32"), ("F0", 128, "bfloat16"), ("Z0", 128, "bfloat16"),
+    for _n, _w, _d in (("WIN", WINW, "bfloat16"), ("EJ", 128, "uint16"), ("PC", 128, "bfloat16"), ("NO", 128, "bfloat16"), ("NP", 128, "bfloat16"),
+                       ("D", 2048, "bfloat16"), ("AB", 2048, "bfloat16"),
+                       ("G", 2048, "bfloat16"), ("MX", 2048, "bfloat16"), ("MN", 2048, "bfloat16"), ("KM", 144, "float32"), ("AA", 256, "float32"),
+                       ("KE", 128, "float32"), ("HIT", 128, "bfloat16"), ("E2", 128, "float32"),
+                       ("EO", 128, "uint16"), ("F0", 128, "bfloat16"), ("Z0", 128, "bfloat16"),
                        ("SLI", 8, "int32"), ("SLA", 8, "int32"), ("SLO", 8, "uint16"), ("DG", 128, "bfloat16"),
-                       ("WLO", 8, "uint16"), ("EG", 128, "float32"), ("BG", 128, "bfloat16"), ("XG", 128, "bfloat16"),
+                       ("WLO", 8, "uint16"), ("BG", 128, "bfloat16"), ("XG", 128, "bfloat16"),
                        ("DD1", 128, "bfloat16"), ("DD2", 128, "bfloat16"), ("AD", 128, "bfloat16"), ("ST", 128, "bfloat16"),
                        ("SX", 128, "bfloat16"), ("SH", 128, "bfloat16"), ("MF", 2048, "bfloat16"), ("NF", 2048, "bfloat16"),
                        ("LF", 128, "float32")):
@@ -66,12 +67,12 @@ def together(big, names):
     SCRATCH[big] = ("sbuf", [128, 128 * len(names)], dtype)
 
 
-together("CB", ["ID", "BT", "BLK", "NROW", "KROW", "KR2", "WA", "WA2", "DK", "IM2", "IP2", "IM1", "I2K", "NBK", "M05", "RK", "IM16", "I64", "IBG",
-                "IT1", "IT2", "IT3", "BS", "BW", "MAD", "V40", "V41", "RS"])
+together("CB", ["ID", "BT", "BLK", "NROW", "KROW", "KR2", "WA", "WA2", "DK", "IH", "IM1", "I2K", "NBK", "M25", "MGC", "RK", "IM16", "I64", "IBG",
+                "IT1", "IT2", "IT3", "BS", "BW", "MAD", "V40", "V41", "DG8"])
 together("CF", ["W1", "W2", "W3", "W4", "W5"])
 for _h in range(2):
-    together("FH%d" % _h, [_n + str(_h) for _n in ("KM", "ZK", "KE", "E2", "EG", "RT", "LF")])
-    together("BH%d" % _h, [_n + str(_h) for _n in ("PC", "NO", "HIT", "F0", "Z0", "DD1", "DD2", "AD", "ST", "SX", "SH")])
+    together("FH%d" % _h, [_n + str(_h) for _n in ("KE", "E2", "LF")])
+    together("BH%d" % _h, [_n + str(_h) for _n in ("PC", "NO", "NP", "HIT", "F0", "Z0", "DD1", "DD2", "AD", "ST", "SX", "SH")])
 for _t in range(3):
     together("ss%d" % _t, ["sa%d" % _t, "sb%d" % _t])
 
@@ -92,13 +93,15 @@ SEMAPHORES = ["cv", "ca", "cp", "cg", "loc"] + ["arr%d" % _t for _t in range(4)]
 CY = 1.0e-3 * 0.95
 GC = 1.5
 SLAT = 0.08
-PARAM_AFTER = []
-AHEAD = 3.0
-WINDOW, SLACK = 0.6, 0.3
-PRIO = {'vDD20': -2.1, 'aZ00': -2.2, 'vMX0.2': -1.3, 'vMN0.2': 6.4, 'vST1': 4.4, 'vEE.3': 3.6, 'aG0.3': -2.0, 'vZK1': 2.1, 'vSLO1': 1.8, 'aAB1.1.1': -11.5, 'aAD1': 3.6, 'asb1': 2.7, 'vMN1.2': -0.6, 'aBG0': 0.2, 'vMN1.1': 0.5, 'asb2': 0.6, 'aW1.g': 1.8, 'vRI': -2.2, 'vD1.0': -5.7, 'vDD10': -0.6, 'vNF1.0': 2.7, 'vXE1.1': -2.2, 'vEE.1': 4.5, 'vSLA1': 3.3, 'aW1.x0': -7.9, 'vMX0.0': 5.4, 'vW1': 0.5, 'vMX1.0': 0.3, 'vZK0': 0.6, 'vMF1.0': 2.0, 'vST0': 0.7, 'pP20': -5.9, 'aAB1.0.0': -4.8, 'aZ01': -0.8, 'aW1.z': 6.4, 'vE21': 4.0, 'aAB0.0.0': -1.0, 'aD0.1': -1.7, 'aAB1.1.0': 0.8, 'vHIT1': 0.1, 'pP10': 0.9, 'aPC1': -9.5, 'vsa2': 1.3, 'vMN0.1': -2.9, 'vRA': 1.0, 'aEG1': -1.3, 'vEG1': 3.8, 'aNO0': -0.4, 'aDG1': 2.2, 'vMX0.1': 0.9, 'vSLI0': 2.9, 'vMX0.3': -0.3, 'vD0.0': -2.6, 'vSX1': -0.1, 'vMX1.1': 0.1, 'vEJ1': 0.5, 'vW0.x0': -4.7, 'vKM0': 5.9, 'vXN.1': -1.8, 'vW0.x1': 2.7, 'vKE0': 2.8, 'aAD0': -9.2, 'vMF0.1': -0.6, 'aG1.3': -0.8, 'vLF0': -0.3, 'aDG0': 1.7, 'aPC0': 0.4, 'aRT0': 3.9, 'vTHR': 1.5, 'vHIT0': 0.3, 'vNF1.1': 0.3, 'vDG0': -0.9, 'vKE1': 1.9, 'vSLA0': 2.2, 'vEE.2': 0.1, 'aRT1': 2.6, 'vG1.0': 6.5, 'vDD11': -0.5}
+AHEAD = 2.0
+WINDOW, SLACK = 0.0, 0.0
+PASSES = 3
+BULK = {}
+PRIO = {"aAB0.1": -1.2, "vMF1.1": -8.4, "aG0.3": -8.6, "vNF0.1": 0.4, "vNF1.0": -8.5, "vDG1": -0.7, "vMX1.1": 7.8, "vMN1.2": 0.5, "vEO0": 3.0}
+BANK = (0, 3, 1, 2)
 BCH = 512
-PARAM = {"judge": [[0, 1], [0, 1]], "bulk": [[[1, 1, 1, 1], [1, 1, 1, 1]], [[0, 1, 1, 1], [0, 1, 1, 1]], [[0, 1, 1, 1], [0, 1, 1, 1]]],
-         "dg": [[1, 1], [1, 1]], "eg": [[1, 1], [1, 0]]}
+PARAM = {"judge": [[1, 0, 1, 0], [0, 1, 1, 1]], "bulk": [[[1, 1, 0, 1], [1, 0, 0, 1]], [[1, 1, 1, 0], [1, 1, 0, 1]], [[1, 0, 1, 1], [1, 1, 0, 1]]],
+         "dg": [[1, 0], [1, 0]]}
 
 
 def build():
@@ -164,7 +167,8 @@ def build():
         return lambda g, T: g.vector.memset(x(T), val)
 
     WX = [["W%d.x%d" % (h, c) for c in range(4)] for h in range(2)]
-    WALL = [WX[h] + ["W%d.g" % h, "W%d.y" % h, "W%d.z" % h] for h in range(2)]
+    WG = [["W%d.g%d" % (h, n) for n in range(2)] for h in range(2)]
+    WALL = [WX[h] + WG[h] + ["W%d.y" % h, "W%d.z" % h] for h in range(2)]
 
     dma("s", lambda g, T: g.sync.dma_start(T.SI[:], T.snd[:]), [], ["SI"], 1.8)
     dma("a", lambda g, T: g.scalar.dma_start(T.WIN0[:, 0:V], T.xa[:]), [], WX[0], 2.2)
@@ -183,7 +187,7 @@ def build():
     vec(lambda g, T: g.vector.tensor_copy(T.sI1[:], T.WIN0[:, 0:V].indirect(T.so4[:, 0:32])), ["so4"] + WX[0], ["sI1"], 60 + 512 * GC)
     act(lambda g, T: g.scalar.activation(T.sI2[:], T.WIN0[:, 0:V].indirect(T.so4[:, 32:64]), F.Copy), ["so4"] + WX[0], ["sI2"], 75 + 512 * GC)
     op("g", ("send", 0, "sI1", "sI2"), ["sI1", "sI2"], ["sent0"], 1.0)
-    op("x", None, ["sent0"], ["W0.g"], 0.0, 1, 5.0, "arr0")
+    op("x", None, ["sent0"], WG[0], 0.0, 1, 5.0, "arr0")
     vec(vcopy(buf("su"), buf("SI")), ["SI"], ["su"], 64)
 
     vec(fill("ONE", 1.0), [], ["ONE"], 512)
@@ -196,20 +200,18 @@ def build():
     vec(fill("O8", 1.0), [], ["O8"], 128)
     gp(lambda g, T: g.affine_select(T.B8T[0:8, :], T.O8[0:8, :], [[1, 128]], A.is_ge, 0.0, 0, -16), ["O8"], ["B8T"], 256)
     gp(lambda g, T: g.affine_select(T.B8[0:8, :], T.B8T[0:8, :], [[-1, 128]], A.is_ge, 0.0, 15, 16), ["B8T"], ["B8"], 256)
-    vec(fill("RMX", 0.0), [], ["RMX"], 512)
-    vec(fill("RMX", -1024.0, 0, 1024, 16), [], ["RMX"], 64)
-    vec(fill("ZX0", 0.0), [], ["ZX0"], 512)
-    act(aact(buf("RMN"), buf("RMX"), F.Copy, 0.0, -1.0), ["RMX"], ["RMN"], 1024)
-    act(aact(buf("M01"), buf("RMX"), F.Identity, 1.0, 1.0 / 1024), ["RMX"], ["M01"], 1024)
-    vec(fill("ZX1", 0.0), [], ["ZX1"], 512)
+    vec(fill("RMX", 0.0), [], ["RMX"], 256)
+    vec(fill("RMX", -1024.0, 0, 512, 16), [], ["RMX"], 64)
+    act(aact(buf("RMN"), buf("RMX"), F.Copy, 0.0, -1.0), ["RMX"], ["RMN"], 512)
     vec(fill("RK", 0.0), [], ["RK"], 64)
     vec(fill("RK", 2097152.0, 0, 128, 16), [], ["RK"], 64)
-    vec(fill("M05", -0.5), [], ["M05"], 64)
+    vec(fill("M25", -0.25, 0, 128), [], ["M25"], 64)
+    vec(fill("MGC", MAGIC, 0, 128), [], ["MGC"], 64)
     vec(fill("O16", 1.0 / 16), [], ["O16"], 128)
     for h in range(2):
-        vec(fill("ZK%d" % h, 0.0), [], ["ZK%d" % h], 128)
+        vec(fill("KM%d" % h, 8388608.0, 128, 144), [], ["KMP%d" % h], 64)
     vec(fill("RS", 0.0), [], ["RS"], 64)
-    vec(fill("RS", -16777216.0, 0, 128, 16), [], ["RS"], 64)
+    vec(fill("RS", -16777216.0, 0, 256, 16), [], ["RS"], 64)
     vec(vts(buf("KI"), buf("PI"), 15, A.bitwise_and), ["PI"], ["KI"], 64)
     vec(vcopy(buf("KC"), buf("KI")), ["KI"], ["KC"], 64)
     vec(vts(buf("G16"), buf("BLK", 0, 128, 16), 16.0, A.mult), ["BLK"], ["G16"], 64)
@@ -233,7 +235,10 @@ def build():
     vec(vtt(buf("WA"), buf("W4"), buf("BLK"), A.mult), ["W4", "BLK"], ["WA"], 256)
     vec(vtt(buf("WA2"), buf("W5"), buf("BLK"), A.mult), ["W5", "BLK"], ["WA2"], 256)
     vec(vts(buf("DK"), buf("ID"), buf("KC"), A.mult), ["ID", "KC"], ["DK"], 128)
-    for nm, val, src in (("IM2", -2.0, "ID"), ("IP2", 2.0, "ID"), ("I64", 65536.0, "ID"), ("IBG", 1048576.0, "ID"), ("IM1", -1.0, "ID"), ("I2K", 2048.0, "ID"), ("IM16", -16.0, "ID"), ("IT1", 1.0, "ID"), ("IT2", 2.0, "ID"), ("IT3", 3.0, "ID"), ("BS", 1024.0, "BLK"), ("NBK", -8192.0, "BLK")):
+    gp(lambda g, T: g.iota(T.PF[:], [[1, 1]], 0, 1, allow_small_or_imprecise_dtypes=True), [], ["PF"], 2)
+    vec(vtt(buf("CC", 20, 21), buf("PF"), buf("KC"), A.subtract), ["PF", "KC"], ["CC5"], 64)
+    vec(vts(buf("DG8"), buf("ID"), 16384.0, A.mult, buf("CC", 20, 21), A.mult), ["ID", "CC5"], ["DG8"], 128)
+    for nm, val, src in (("IH", 0.5, "ID"), ("I64", 65536.0, "ID"), ("IBG", 1048576.0, "ID"), ("IM1", -1.0, "ID"), ("I2K", 2048.0, "ID"), ("IM16", -16.0, "ID"), ("IT1", 1.0, "ID"), ("IT2", 2.0, "ID"), ("IT3", 3.0, "ID"), ("BS", 1024.0, "BLK"), ("NBK", -8192.0, "BLK")):
         act(aact(buf(nm), buf(src), F.Copy, 0.0, val), [src], [nm], 128)
     vec(vcopy(buf("THF"), buf("TH8")), ["TH8"], ["THF"], 64)
     pe(mms([(buf("P30", 0, 4), lambda T: T.B8[0:8, :], lambda T: T.THF[:], True, True)]), ["B8", "THF"], ["P30"], 256, 1)
@@ -264,28 +269,31 @@ def build():
     def cls(t, h):
         return t + 512 * h, 512 * h + 512, 4
 
-    def prep(t):
-        for h in range(2):
-            a, b, s = cls(t, h)
-            H = "%d" % h
-            for c in range(2):
-                vec(vcopy(buf("ZX" + H, 0, 1024, 16), buf("WIN0", a + 256 * c, 512 * h + 256 * c + 256, s)), ["W0.x%d" % t, "ZX" + H], ["ZX" + H], 64)
-                vec(lambda g, T, H=H, c=c: g.vector.tensor_tensor_scan(T["XE" + H][:, 1024 * c:1024 * c + 1024], T.M01[:], T["ZX" + H][:], 0.0, A.mult, A.add),
-                    ["M01", "ZX" + H], ["XE%s.%d" % (H, c)], 512)
-            vec(vcopy(buf("EJ" + H), buf("EI", a, b, s)), ["EI"], ["EJ" + H], 128)
-            act(aact(buf("PC" + H), buf("EE", a, b, s), F.Sign, -2047.5), ["EE.%d" % t], ["PC" + H], 128)
-            pe(mms([(buf("P0" + H, 128, 256), buf("BLK"), buf("PC" + H), True, True)]), ["BLK", "PC" + H], ["P0" + H], 128, 1)
-            act(aact(buf("NO" + H), buf("P0" + H, 128, 256), F.Relu, -15.0), ["P0" + H], ["NO" + H], 128)
+    def clean(t, h):
+        a, b, s = cls(t, h)
+        H = "%d" % h
+        vec(vcopy(buf("EJ" + H), buf("EI", a, b, s)), ["EI"], ["EJ" + H], 128)
+        act(aact(buf("PC" + H), buf("EE", a, b, s), F.Sign, -2047.5), ["EE.%d" % t], ["PC" + H], 128)
+        pe(mms([(buf("P0" + H, 128, 256), buf("BLK"), buf("PC" + H), True, True)]), ["BLK", "PC" + H], ["P0" + H], 128, 1)
+        act(aact(buf("%s%d" % ("NO" if t % 2 else "NP", h)), buf("P0" + H, 128, 256), F.Relu, -15.0), ["P0" + H], ["NO%d.%d" % (t % 2, h)], 128)
 
-    prep(0)
-    act(lambda g, T: g.scalar.activation(T.WIN1[:, 1024:2048], T.WIN0[:, 1024:2048], F.Copy), ["W0.g"], ["W1.g"], 1024)
+    def minus(t, h, c):
+        a, pb = t + 512 * h + 128 * c, "P%d%d" % (BANK[c], h)
+        for j in range(0, 16, 4):
+            pe(mms([(buf(pb, k, 512, 16), buf("IM1"), buf("WIN0", a, a + 128 - t, 4), k == 0, False) for k in range(j, j + 4)]),
+               ["IM1", "W0.x%d" % t], [pb], 256, 4)
+
+    for h in range(2):
+        clean(0, h)
+        for c in range(4):
+            minus(0, h, c)
+    act(lambda g, T: g.scalar.activation(T.WIN1[:, 1024:2048], T.WIN0[:, 1024:2048], F.Copy), WG[0], WG[1], 1024)
     for h in range(2):
         vec(fill("WIN%d" % h, 0.0, 4096, 4224), [], ["W%d.z" % h], 64)
 
     def rounding(h, bank, out, outkey):
         H = "%d" % h
-        act(aact(buf("RT" + H), buf(bank, 0, 128), F.Identity, MAGIC, 0.5), [bank], ["RT" + H], 128)
-        act(aact(out, buf("RT" + H), F.Abs, -MAGIC, 1.0), ["RT" + H], [outkey], 128)
+        act(aact(out, buf(bank, 0, 128), F.Abs, -MAGIC, 1.0), [bank], [outkey], 128)
 
     def scans(h, src, c, n, mx="MX", mn="MN"):
         H = "%d" % h
@@ -300,17 +308,15 @@ def build():
         else:
             vec(lambda g, T: g.vector.tensor_copy(fout(T), fsrc(T)), r, w, 60 + 128 * GC)
 
-    def fmm(h, bank, bsrc, bkey, extra=(), mx="MX", mn="MN"):
+    def fmm(h, bank, bsrc, bkey, mx="MX", mn="MN"):
         H = "%d" % h
-        st = [(buf(bank, 0, 128), buf("ID"), buf("M05"), True, False), (buf(bank, 0, 128), buf("IM2"), bsrc, False, False)]
-        rk = ["ID", "M05", "IM2", bkey]
-        for c, src, key in extra:
-            st.append((buf(bank, 64 * c, 64 * c + 64), buf("IP2"), src, False, False))
-            rk += ["IP2", key]
+        st = [(buf(bank, 0, 128), buf("ID"), buf("M25"), True, False), (buf(bank, 0, 128), buf("IM1"), bsrc, False, False)]
+        rk = ["ID", "M25", "IM1", bkey]
         pe(mms(st), rk, [bank], 128 * len(st), len(st))
-        ks = ["%s%d.%d" % (m, h, c) for m in (mx, mn) for c in range(2 if mx == "MF" else 2048 // BCH)]
-        pe(mms([(buf(bank, 0, 128), buf("ID"), buf(mx + H, 15, 2048, 16), False, False),
-                (buf(bank, 0, 128), buf("ID"), buf(mn + H, 15, 2048, 16), False, True)]), ["ID"] + ks, [bank], 256, 2)
+        kx, kn = [["%s%d.%d" % (m, h, c) for c in range(2048 // BCH)] for m in (mx, mn)]
+        pe(mms([(buf(bank, 0, 128), buf("IH"), buf(mx + H, 15, 2048, 16), False, False)]), ["IH"] + kx, [bank], 128, 1)
+        pe(mms([(buf(bank, 0, 128), buf("IH"), buf(mn + H, 15, 2048, 16), False, False),
+                (buf(bank, 0, 128), buf("ID"), buf("MGC"), False, True)]), ["ID", "IH", "MGC"] + kn, [bank], 256, 2)
 
     def bulk(h, hop):
         H = "%d" % h
@@ -324,9 +330,9 @@ def build():
         for c in range(2048 // BCH):
             scans(h, "G" + H, c, BCH)
 
-    def diagonal(h, bank):
+    def diagonal(h, bank, a=0):
         H = "%d" % h
-        vec(lambda g, T: g.vector.tensor_tensor_scan(cols(T, "LF" + H), cols(T, "RS"), T[bank][:, 0:128], 0.0, A.add, A.max),
+        vec(lambda g, T: g.vector.tensor_tensor_scan(cols(T, "LF" + H), T.RS[:, 0:128], T[bank][:, a:a + 128], 0.0, A.add, A.max),
             ["RS", bank], ["LF" + H], 128)
 
     for t in range(RO):
@@ -334,43 +340,39 @@ def build():
             half[0] = h
             H = "%d" % h
             a, b, s = cls(t, h)
-            for c in range(2):
-                p, q = 1024 * c, 1024 * c + 1024
-                src = ind("WIN" + H, 0, WINW, "EJ" + H, 64 * c, 64 * c + 64)
-                rk, dk, ak = WALL[h] + ["EJ" + H], "D%d.%d" % (h, c), "AB%d.%d" % (h, c)
+            for c in range(4):
+                p, q, pb = 512 * c, 512 * c + 512, "P%d%s" % (BANK[c], H)
+                src = ind("WIN" + H, 0, 4096, "EJ" + H, 32 * c, 32 * c + 32)
+                rk, dk, ak = WALL[h][:-1] + ["EJ" + H], "D%d.%d" % (h, c), "AB%d.%d" % (h, c)
                 if PARAM["judge"][h][c]:
-                    act(lambda g, T, o=buf("D" + H, p, q), s=src: g.scalar.activation(o(T), s(T), F.Copy), rk, [dk], 75 + 1024 * GC)
-                    for j in range(2):
-                        u, w, pb = p + 512 * j, p + 512 * j + 512, "P%d%s" % (3 - 2 * j, H)
-                        pe(mms([(buf(pb), buf("IM1"), buf("XE" + H, u, w), True, False), (buf(pb), buf("ID"), buf("D" + H, u, w), False, True)]),
-                           ["IM1", "ID", dk, "XE%s.%d" % (H, c)], [pb], 1024, 2)
-                        act(aact(buf("AB" + H, u, w), buf(pb), F.Abs), [pb], ["%s.%d" % (ak, j)], 512)
+                    act(lambda g, T, o=buf("D" + H, p, q), s=src: g.scalar.activation(o(T), s(T), F.Copy), rk, [dk], 75 + 512 * GC)
                 else:
-                    vec(lambda g, T, o=buf("D" + H, p, q), s=src, x=buf("XE" + H, p, q): g.vector.tensor_tensor(o(T), s(T), x(T), A.subtract),
-                        rk + ["XE%s.%d" % (H, c)], [dk], 60 + 1024 * GC)
-                    act(aact(buf("AB" + H, p, q), buf("D" + H, p, q), F.Abs), [dk], [ak + ".0", ak + ".1"], 1024)
+                    vec(lambda g, T, o=buf("D" + H, p, q), s=src: g.vector.tensor_copy(o(T), s(T)), rk, [dk], 60 + 512 * GC)
+                pe(mms([(buf(pb), buf("ID"), buf("D" + H, p, q), False, True)]), ["ID", dk], [pb], 512, 1)
+                act(aact(buf("AB" + H, p, q), buf(pb), F.Abs), [pb], [ak], 512)
             pe(mms([(buf("P0" + H, 0, 128), buf("PC" + H), buf("I64"), True, False),
-                    (buf("P0" + H, 0, 128), buf("ONE", 0, 128), buf("DK"), False, False)]), ["PC" + H, "I64", "ONE", "DK"], ["P0" + H], 256, 2)
+                    (buf("P0" + H, 0, 128), buf("ONE", 0, 128), buf("DK"), False, False), (buf("P0" + H, 0, 128), buf("ONE", 0, 128), buf("DG8"), False, False)]),
+               ["PC" + H, "I64", "ONE", "DK", "DG8"], ["P0" + H], 384, 3)
             pe(mms([(buf("P0" + H, k, 128, 16), buf("AB" + H, k, 2048, 16), buf("G16"), False, k == 15) for k in range(16)]),
-               ["AB%d.%d.%d" % (h, c, j) for c in range(2) for j in range(2)] + ["G16"], ["P0" + H], 1024, 16)
-            vec(lambda g, T, H=H: g.vector.tensor_tensor_scan(cols(T, "KM" + H), cols(T, "RK"), T["P0" + H][:, 0:128], 0.0, A.add, A.min),
-                ["RK", "P0" + H], ["KM" + H], 128)
-            vec(vcopy(buf("ZK" + H, 0, 128, 16), buf("KM" + H, 15, 128, 16)), ["KM" + H, "ZK" + H], ["ZK" + H], 64)
-            vec(lambda g, T, H=H: g.vector.tensor_tensor_scan(cols(T, "KE" + H), T.M01[:, 0:128], cols(T, "ZK" + H), 0.0, A.mult, A.add),
-                ["M01", "ZK" + H], ["KE" + H], 128)
+               ["AB%d.%d" % (h, c) for c in range(4)] + ["G16"], ["P0" + H], 1024, 16)
+            vec(lambda g, T, H=H: g.vector.tensor_tensor_scan(T["KM" + H][:, 0:128], cols(T, "RK"), T["P0" + H][:, 0:128], 0.0, A.add, A.min),
+                ["RK", "P0" + H, "KMP" + H], ["KM" + H], 128)
+            vec(lambda g, T, H=H: g.vector.tensor_tensor_scan(cols(T, "KE" + H), cols(T, "RK"), T["KM" + H][:, 15:143], 0.0, A.add, A.min),
+                ["RK", "KM" + H, "KMP" + H], ["KE" + H], 128)
             vec(vtt(buf("HIT" + H), buf("P0" + H, 0, 128), buf("KE" + H), A.is_equal), ["P0" + H, "KE" + H], ["HIT" + H], 128)
             pe(mms([(buf("P1" + H, 0, 128), buf("HIT" + H), buf("I2K"), True, True)]), ["HIT" + H, "I2K"], ["P1" + H], 128, 1)
             vec(vtt(buf("E2" + H), buf("EI", a, b, s), buf("P1" + H, 0, 128), A.add), ["EI", "P1" + H], ["E2" + H], 128)
             vec(vts(buf("EO" + H), buf("E2" + H), 4095.0, A.min), ["E2" + H], ["EO" + H], 128)
-            xv = [(c, buf("WIN" + H, a + 256 * c, 256 * c + 512 * h + 256, s), "W%d.x%d" % (h, t)) for c in range(2) if not PARAM["judge"][h][c]]
-            for c in range(2):
-                scans(h, "D" + H, c, 1024, "MF", "NF")
-            fmm(h, "P2" + H, buf("BN", a, b, s), "BN", xv, "MF", "NF")
+            if t < RO - 1:
+                clean(t + 1, h)
+            for c in range(2048 // BCH):
+                scans(h, "D" + H, c, BCH, "MF", "NF")
+            fmm(h, "P2" + H, buf("BN", a, b, s), "BN", "MF", "NF")
             rounding(h, "P2" + H, buf("F0" + H), "F0" + H)
             bulk(h, 0)
             fmm(h, "P3" + H, buf("BN", a, b, s), "BN")
             rounding(h, "P3" + H, buf("WIN" + H, 4096, 4224), "W%d.z" % h)
-            act(aact(buf("Z0" + H), buf("RT" + H), F.Abs, -MAGIC, 1.0), ["RT" + H], ["Z0" + H], 128)
+            rounding(h, "P3" + H, buf("Z0" + H), "Z0" + H)
             for hop in (1, 2):
                 p0 = buf("P0" + H, 0, 128)
                 st, rk = [(p0, buf("ID"), buf("MAD"), True, False)], ["ID", "MAD"]
@@ -396,15 +398,16 @@ def build():
                         (buf("P2" + H, 128, 256), buf("WA2"), buf("DG" + H), True, True)]), ["ID", "NROW", "WA", "WA2", "DG" + H], ["P2" + H], 384, 3)
                 diagonal(h, "P1" + H)
                 vec(vcopy(buf("WLO" + H), buf("LF" + H, 15, 128, 16)), ["LF" + H], ["WLO" + H], 64)
-                small(PARAM["eg"][hop - 1][h], buf("EG" + H), ind("EE", 0, 1024, "WLO" + H, 0, 8), EEK + ["WLO" + H], ["EG" + H])
-                vec(vtt(buf("E2" + H), buf("EG" + H), buf("P2" + H, 0, 128), A.max), ["EG" + H, "P2" + H], ["E2" + H], 128)
+                act(aact(buf("AA" + H, 0, 256), buf("P2" + H, 0, 256), F.Copy), ["P2" + H], ["AA" + H], 256)
+                eg = ind("EE", 0, 1024, "WLO" + H, 0, 8)
+                vec(vtt(buf("E2" + H), eg, buf("AA" + H, 0, 128), A.max), EEK + ["WLO" + H, "AA" + H], ["E2" + H], 60 + 128 * GC)
                 vec(vcopy(buf("EO" + H), buf("E2" + H)), ["E2" + H], ["EO" + H], 128)
                 act(lambda g, T, H=H: g.scalar.activation(T["BG" + H][:], T.BN[:, 0:1024].indirect(T["WLO" + H][:, 0:8]), F.Copy),
                     ["BN", "WLO" + H], ["BG" + H], 75 + 128 * GC)
                 if hop == 2:
                     act(lambda g, T, H=H: g.scalar.activation(T["XG" + H][:], T["WIN" + H][:, 0:1024].indirect(T["WLO" + H][:, 0:8]), F.Copy),
                         WX[h] + ["WLO" + H], ["XG" + H], 75 + 128 * GC)
-                vec(vtt(buf("DD%d%d" % (hop, h)), buf("EG" + H), buf("P2" + H, 128, 256), A.is_ge), ["EG" + H, "P2" + H], ["DD%d%d" % (hop, h)], 128)
+                vec(vtt(buf("DD%d%d" % (hop, h)), eg, buf("AA" + H, 128, 256), A.is_ge), EEK + ["WLO" + H, "AA" + H], ["DD%d%d" % (hop, h)], 60 + 128 * GC)
                 bulk(h, hop)
                 fmm(h, "P3" + H, buf("BG" + H), "BG" + H)
                 rounding(h, "P3" + H, buf("WIN" + H, 4096, 4224), "W%d.z" % h)
@@ -412,14 +415,14 @@ def build():
             pe(mms([(buf("P3" + H, 0, 128), buf("ID"), buf("WIN" + H, 4096, 4224), False, True)]), ["ID", "W%d.z" % h], ["P3" + H], 128, 1)
             act(aact(buf("AD" + H), buf("P3" + H, 0, 128), F.Abs), ["P3" + H], ["AD" + H], 128)
             pe(mms([(buf("P2" + H, 0, 128), buf("ID"), buf("Z0" + H), True, False), (buf("P2" + H, 0, 128), buf("IM1"), buf("F0" + H), False, True),
-                    (buf("P2" + H, 128, 256), buf("HIT" + H), buf("I2K"), True, True)]),
-               ["ID", "IM1", "I2K", "Z0" + H, "F0" + H, "HIT" + H], ["P2" + H], 384, 3)
-            pe(mms([(buf("P1" + H, 0, 128), buf("IBG"), buf("NO" + H), True, False), (buf("P1" + H, 0, 128), buf("NBK"), buf("DD1" + H), False, False),
-                    (buf("P1" + H, 0, 128), buf("NBK"), buf("DD2" + H), False, False)]), ["IBG", "NO" + H, "NBK", "DD1" + H, "DD2" + H], ["P1" + H], 384, 3)
+                    (buf("P2" + H, 128, 256), buf("HIT" + H), buf("I2K"), True, True), (buf("P2" + H, 384, 512), buf("ID"), buf("F0" + H), True, True)]),
+               ["ID", "IM1", "I2K", "Z0" + H, "F0" + H, "HIT" + H], ["P2" + H], 512, 4)
+            pe(mms([(buf("P1" + H, 0, 128), buf("IBG"), buf(("NO" if t % 2 else "NP") + H), True, False), (buf("P1" + H, 0, 128), buf("NBK"), buf("DD1" + H), False, False),
+                    (buf("P1" + H, 0, 128), buf("NBK"), buf("DD2" + H), False, False)]), ["IBG", "NO%d.%d" % (t % 2, h), "NBK", "DD1" + H, "DD2" + H], ["P1" + H], 384, 3)
             pe(mms([(buf("P1" + H, 0, 128), buf("BLK"), buf("AD" + H), False, True)]), ["BLK", "AD" + H], ["P1" + H], 128, 1)
             vec(vts(buf("ST" + H), buf("P1" + H, 0, 128), buf("THR", t, t + 1), A.is_le), ["P1" + H, "THR"], ["ST" + H], 128)
             vec(vtt(buf("SX" + H), buf("ST" + H), buf("P2" + H, 0, 128), A.mult), ["ST" + H, "P2" + H], ["SX" + H], 128)
-            vec(vtt(buf("XN", 128 * h, 128 * h + 128), buf("F0" + H), buf("SX" + H), A.add), ["F0" + H, "SX" + H], ["XN.%d" % h], 256)
+            vec(vtt(buf("XN", 128 * h, 128 * h + 128), buf("P2" + H, 384, 512), buf("SX" + H), A.add), ["P2" + H, "SX" + H], ["XN.%d" % h], 128)
         half[0] = 1
         XNK = ["XN.0", "XN.1"]
         if t < RO - 1:
@@ -435,8 +438,8 @@ def build():
             H = "%d" % h
             a, b, s = cls(t, h)
             vec(vtt(buf("SH" + H), buf("ST" + H), buf("P2" + H, 128, 256), A.mult), ["ST" + H, "P2" + H], ["SH" + H], 128)
-            pe(mms([(buf("P3" + H, 0, 128), buf("ID"), buf("SH" + H), True, True)]), ["ID", "SH" + H], ["P3" + H], 128, 1)
-            vec(vtt(buf("EE", a, b, s), buf("EI", a, b, s), buf("P3" + H, 0, 128), A.add), ["EI", "P3" + H], ["EE.%d" % t], 128)
+            pe(mms([(buf("P2" + H, 256, 384), buf("ID"), buf("SH" + H), True, True)]), ["ID", "SH" + H], ["P2" + H], 128, 1)
+            vec(vtt(buf("EE", a, b, s), buf("EI", a, b, s), buf("P2" + H, 256, 384), A.add), ["EI", "P2" + H], ["EE.%d" % t], 128)
         if t == RO - 1:
             dma("a", lambda g, T: g.scalar.dma_start(T.ye[:], T.EE[:]), EEK, [], 2.0)
         else:
@@ -444,22 +447,22 @@ def build():
                 H = "%d" % h
                 act(lambda g, T, H=H, h=h: g.scalar.activation(cols(T, "AD" + H), cols(T, "ST" + H), F.Copy, accum_out=T.CNT[:, h:h + 1]),
                     ["ST" + H], ["CNT", "AD" + H], 150)
-            pe(mms([(buf("P30", 0, 2), buf("O16"), buf("CNT"), True, True)]), ["O16", "CNT"], ["P30"], 256, 1)
-            vec(vcopy(buf("W1", 0, 2), buf("P30", 0, 2)), ["P30"], ["W1"], 64)
+            pe(mms([(buf("P20", 384, 386), buf("O16"), buf("CNT"), True, True)]), ["O16", "CNT"], ["P20"], 256, 1)
+            vec(vcopy(buf("W1", 0, 2), buf("P20", 384, 386)), ["P20"], ["W1"], 64)
             vec(vtt(buf("RI"), buf("W1", 0, 1), buf("W1", 1, 2), A.add), ["W1"], ["RI"], 64)
             vec(vts(buf("RA"), buf("RI"), 31, A.bitwise_and), ["RI"], ["RA"], 64)
             vec(vtt(buf("THR", t + 1, t + 2), buf("THC", t + 1, t + 2), buf("RA"), A.add), ["THC", "RA"], ["THR"], 64)
-            after.extend(PARAM_AFTER)
-            prep(t + 1)
-            del after[:]
+            for c in range(4):
+                for h in range(2):
+                    minus(t + 1, h, c)
             for h in range(2):
                 for n in range(2):
                     a = 1024 + 512 * n + 128 * t
                     o, i = buf("WIN%d" % h, a, a + 128), buf("la%d" % t, 128 * n, 128 * n + 128)
-                    if h:
-                        act(aact(o, i, F.Copy), ["la%d" % t], ["W1.g"], 128)
+                    if n:
+                        act(aact(o, i, F.Copy), ["la%d" % t], ["W%d.g%d" % (h, n)], 128)
                     else:
-                        vec(vcopy(o, i), ["la%d" % t], ["W0.g"], 64)
+                        vec(vcopy(o, i), ["la%d" % t], ["W%d.g%d" % (h, n)], 64)
     return ops
 
 
@@ -520,8 +523,55 @@ def schedule(ops, pred):
         o = ops[i]
         if o["h"] == 0:
             prio[i] += AHEAD
+        if o["w"] and o["w"][0][:2] in BULK:
+            prio[i] -= BULK[o["w"][0][:2]]
         if o["w"]:
             prio[i] += PRIO.get(o["q"] + o["w"][0], 0.0)
+    best = forward(ops, pred, succ, prio)
+    res, stale = best, 0
+    for _ in range(PASSES):
+        late = backward(ops, pred, succ, res)
+        res = forward(ops, pred, succ, [-x for x in late])
+        if max(res[2]) < max(best[2]) - 1e-9:
+            best = res
+    return best
+
+
+def backward(ops, pred, succ, res):
+    n = len(ops)
+    fin = res[2]
+    left = [len(succ[i]) for i in range(n)]
+    at, free, late, done = [0.0] * n, {}, [0.0] * n, 0
+    ready = {}
+    for i in range(n):
+        if left[i] == 0:
+            ready.setdefault(ops[i]["q"], []).append(i)
+    while done < n:
+        best = None
+        for q, lst in ready.items():
+            if not lst:
+                continue
+            s = max(free.get(q, 0.0), min(at[i] for i in lst))
+            i = max((i for i in lst if at[i] <= s + 1e-9), key=lambda i: (fin[i], i))
+            if best is None or s < best[0]:
+                best = (s, q, i)
+        s, q, i = best
+        ready[q].remove(i)
+        e = s + ops[i]["cost"]
+        free[q] = e if q != "x" else 0.0
+        late[i] = -e
+        done += 1
+        for j in pred[i]:
+            at[j] = max(at[j], e + (SLAT if pred[i][j] else 0.0) + ops[j]["lat"])
+            left[j] -= 1
+            if left[j] == 0:
+                ready.setdefault(ops[j]["q"], []).append(j)
+    return late
+
+
+def forward(ops, pred, succ, prio):
+    n = len(ops)
+    LAT = SLAT
     left = [len(pred[i]) for i in range(n)]
     ready = {}
     at = [0.0] * n

import numpy as np
from concourse.bass import DstId, RemoteDMATransfer
from concourse.mybir import AluOpType as A, AxisListType, ActivationFunctionType as F

V, NCL, RO = 1024, 4, 4
WINW = 4096 + 128
MAGIC = 12582912.0

SCRATCH = {
    "EI": ("sbuf", [128, 1024], "int32"), "EE": ("sbuf", [128, 1024], "float32"), "UI": ("sbuf", [128, 1024], "int32"),
    "UT": ("sbuf", [128, 1024], "int32"), "BN": ("sbuf", [128, 1024], "bfloat16"), "SI": ("sbuf", [128, 64], "int32"),
    "dg0": ("sbuf", [128, 1024], "bfloat16"), "dg1": ("sbuf", [128, 1024], "bfloat16"),
    "dg2": ("sbuf", [128, 1024], "bfloat16"), "dg3": ("sbuf", [128, 1024], "bfloat16"),
    "Ud": ("sbuf", [128, 16384], "bfloat16"), "ONE": ("sbuf", [128, 1024], "bfloat16"),
    "CI": ("sbuf", [128, 64], "int32"), "S4": ("sbuf", [128, 64], "int32"), "S5": ("sbuf", [128, 64], "int32"),
    "so4": ("sbuf", [128, 64], "uint16"), "su": ("sbuf", [128, 64], "uint16"),
    "ID": ("sbuf", [128, 128], "bfloat16"), "BT": ("sbuf", [128, 128], "bfloat16"), "BLK": ("sbuf", [128, 128], "bfloat16"),
    "NROW": ("sbuf", [128, 128], "bfloat16"), "KROW": ("sbuf", [128, 128], "bfloat16"), "KR2": ("sbuf", [128, 128], "bfloat16"),
    "PI": ("sbuf", [128, 1], "int32"), "KI": ("sbuf", [128, 1], "int32"), "KC": ("sbuf", [128, 1], "float32"),
    "O8": ("sbuf", [128, 128], "float32"), "B8T": ("sbuf", [128, 128], "float32"), "B8": ("sbuf", [128, 128], "float32"),
    "G16": ("sbuf", [128, 8], "bfloat16"),
    "CC": ("sbuf", [128, 64], "float32"), "W1": ("sbuf", [128, 128], "float32"), "W2": ("sbuf", [128, 128], "float32"),
    "W3": ("sbuf", [128, 128], "float32"), "W4": ("sbuf", [128, 128], "float32"), "W5": ("sbuf", [128, 128], "float32"),
    "WA": ("sbuf", [128, 128], "bfloat16"), "WA2": ("sbuf", [128, 128], "bfloat16"), "DK": ("sbuf", [128, 128], "bfloat16"),
    "IH": ("sbuf", [128, 128], "bfloat16"), "MGC": ("sbuf", [128, 128], "bfloat16"), "IM1": ("sbuf", [128, 128], "bfloat16"),
    "I2K": ("sbuf", [128, 128], "bfloat16"), "NBK": ("sbuf", [128, 128], "bfloat16"), "M25": ("sbuf", [128, 128], "bfloat16"),
    "O16": ("sbuf", [128, 128], "float32"), "RK": ("sbuf", [128, 128], "bfloat16"),
    "RMX": ("sbuf", [128, 512], "bfloat16"), "RMN": ("sbuf", [128, 512], "bfloat16"),
    "dgL": ("sbuf", [128, 1024], "bfloat16"), "IM16": ("sbuf", [128, 128], "bfloat16"),
    "I64": ("sbuf", [128, 128], "bfloat16"), "IBG": ("sbuf", [128, 128], "bfloat16"), "RS": ("sbuf", [128, 256], "bfloat16"), "DG8": ("sbuf", [128, 128], "bfloat16"), "PF": ("sbuf", [128, 1], "float32"),

    "IT1": ("sbuf", [128, 128], "bfloat16"), "IT2": ("sbuf", [128, 128], "bfloat16"), "IT3": ("sbuf", [128, 128], "bfloat16"),
    "BS": ("sbuf", [128, 128], "bfloat16"), "BW": ("sbuf", [128, 128], "bfloat16"), "MAD": ("sbuf", [128, 128], "bfloat16"),
    "V40": ("sbuf", [128, 128], "bfloat16"), "V41": ("sbuf", [128, 128], "bfloat16"),
    "TH8": ("sbuf", [8, 4], "int32"), "THF": ("sbuf", [8, 4], "float32"), "THC": ("sbuf", [128, 4], "float32"),
    "RI": ("sbuf", [128, 1], "int32"), "RA": ("sbuf", [128, 1], "int32"), "THR": ("sbuf", [128, 4], "float32"),
    "CNT": ("sbuf", [128, 2], "float32"), "XN": ("sbuf", [128, 256], "bfloat16"),
    "sI1": ("sbuf", [128, 512], "bfloat16"), "sI2": ("sbuf", [128, 512], "bfloat16"),
}
for _h in range(2):
    for _n, _w, _d in (("WIN", WINW, "bfloat16"), ("EJ", 128, "uint16"), ("PC", 128, "bfloat16"), ("NO", 128, "bfloat16"), ("NP", 128, "bfloat16"),
                       ("D", 2048, "bfloat16"), ("AB", 2048, "bfloat16"),
                       ("G", 2048, "bfloat16"), ("MX", 2048, "bfloat16"), ("MN", 2048, "bfloat16"), ("KM", 144, "float32"), ("AA", 256, "float32"),
                       ("KE", 128, "float32"), ("HIT", 128, "bfloat16"), ("E2", 128, "float32"),
                       ("EO", 128, "uint16"), ("F0", 128, "bfloat16"), ("Z0", 128, "bfloat16"),
                       ("SLI", 8, "int32"), ("SLA", 8, "int32"), ("SLO", 8, "uint16"), ("DG", 128, "bfloat16"),
                       ("WLO", 8, "uint16"), ("BG", 128, "bfloat16"), ("XG", 128, "bfloat16"),
                       ("DD1", 128, "bfloat16"), ("DD2", 128, "bfloat16"), ("AD", 128, "bfloat16"), ("ST", 128, "bfloat16"),
                       ("SX", 128, "bfloat16"), ("SH", 128, "bfloat16"), ("MF", 2048, "bfloat16"), ("NF", 2048, "bfloat16"),
                       ("LF", 128, "float32")):
        SCRATCH["%s%d" % (_n, _h)] = ("sbuf", [128, _w], _d)
    for _b in range(4):
        SCRATCH["P%d%d" % (_b, _h)] = ("psum", [128, 512], "float32")
for _t in range(3):
    SCRATCH["la%d" % _t] = ("sbuf", [128, 256], "bfloat16")
    SCRATCH["sa%d" % _t] = ("sbuf", [128, 128], "bfloat16")
    SCRATCH["sb%d" % _t] = ("sbuf", [128, 128], "bfloat16")

ALIAS = {}


def together(big, names):
    dtype = SCRATCH[names[0]][2]
    for k, nm in enumerate(names):
        ALIAS[nm] = (big, 128 * k)
        del SCRATCH[nm]
    SCRATCH[big] = ("sbuf", [128, 128 * len(names)], dtype)


together("CB", ["ID", "BT", "BLK", "NROW", "KROW", "KR2", "WA", "WA2", "DK", "IH", "IM1", "I2K", "NBK", "M25", "MGC", "RK", "IM16", "I64", "IBG",
                "IT1", "IT2", "IT3", "BS", "BW", "MAD", "V40", "V41", "DG8"])
together("CF", ["W1", "W2", "W3", "W4", "W5"])
for _h in range(2):
    together("FH%d" % _h, [_n + str(_h) for _n in ("KE", "E2", "LF")])
    together("BH%d" % _h, [_n + str(_h) for _n in ("PC", "NO", "NP", "HIT", "F0", "Z0", "DD1", "DD2", "AD", "ST", "SX", "SH")])
for _t in range(3):
    together("ss%d" % _t, ["sa%d" % _t, "sb%d" % _t])


def cols(T, name, a=0, b=None, s=1):
    if name in ALIAS:
        big, o = ALIAS[name]
        b = 128 if b is None else b
        return T[big][:, o + a:o + b:s] if s != 1 else T[big][:, o + a:o + b]
    if b is None:
        return T[name][:]
    return T[name][:, a:b:s] if s != 1 else T[name][:, a:b]


NDMA = 40
SEMAPHORES = ["cv", "ca", "cp", "cg", "loc"] + ["arr%d" % _t for _t in range(4)] + ["dm%d" % _t for _t in range(NDMA)]

CY = 1.0e-3 * 0.95
GC = 1.5
SLAT = 0.08
AHEAD = 2.0
WINDOW, SLACK = 0.0, 0.0
PASSES = 3
BULK = {}
PRIO = {"aAB0.1": -1.2, "vMF1.1": -8.4, "aG0.3": -8.6, "vNF0.1": 0.4, "vNF1.0": -8.5, "vDG1": -0.7, "vMX1.1": 7.8, "vMN1.2": 0.5, "vEO0": 3.0}
BANK = (0, 3, 1, 2)
BCH = 512
PARAM = {"judge": [[1, 0, 1, 0], [0, 1, 1, 1]], "bulk": [[[1, 1, 0, 1], [1, 0, 0, 1]], [[1, 1, 1, 0], [1, 1, 0, 1]], [[1, 0, 1, 1], [1, 1, 0, 1]]],
         "dg": [[1, 0], [1, 0]]}


def build():
    ops = []
    ndma = [0]
    half = [1]
    after = []

    def op(q, fn, r, w, cost, n=1, lat=0.0, sem=None):
        ops.append({"q": q, "fn": fn, "r": r, "w": w, "cost": cost, "n": n, "lat": lat, "sem": sem, "i": len(ops), "after": after[:],
                    "h": half[0]})

    def vec(fn, r, w, cyc):
        op("v", fn, r, w, max(64, cyc) * CY + 0.02)

    def act(fn, r, w, cyc):
        op("a", fn, r, w, max(64, cyc) * CY + 0.02)

    def pe(fn, r, w, cyc, n):
        op("p", fn, r, w, cyc * CY, n)

    def gp(fn, r, w, cyc):
        op("g", fn, r, w, cyc * CY + 0.15)

    def dma(q, fn, r, w, lat):
        op(q, fn, r, w, 0.06, 1, lat, "dm%d" % ndma[0])
        ndma[0] += 1

    def vcopy(o, i):
        return lambda g, T: g.vector.tensor_copy(o(T), i(T))

    def vts(o, i, s1, o1, s2=None, o2=None):
        def fn(g, T):
            a = s1(T) if callable_(s1) else s1
            if o2 is None:
                return g.vector.tensor_scalar(o(T), i(T), a, None, o1)
            b = s2(T) if callable_(s2) else s2
            return g.vector.tensor_scalar(o(T), i(T), a, b, o1, o2)
        return fn

    def callable_(x):
        return not isinstance(x, (int, float))

    def vtt(o, a, b, f):
        return lambda g, T: g.vector.tensor_tensor(o(T), a(T), b(T), f)

    def aact(o, i, f, bias=0.0, scale=1.0):
        return lambda g, T: g.scalar.activation(o(T), i(T), f, bias=bias, scale=scale)

    def buf(name, a=None, b=None, s=1):
        return lambda T: cols(T, name, a or 0, b, s)

    def ind(name, a, b, off, c, d):
        return lambda T: T[name][:, a:b].indirect(T[off][:, c:d])

    def mms(lst):
        def fn(g, T):
            return [g.tensor.matmul(o(T), l(T), r(T), s, e) for o, l, r, s, e in lst]
        return fn

    def fill(name, val, a=None, b=None, s=1):
        x = buf(name, a, b, s)
        return lambda g, T: g.vector.memset(x(T), val)

    WX = [["W%d.x%d" % (h, c) for c in range(4)] for h in range(2)]
    WG = [["W%d.g%d" % (h, n) for n in range(2)] for h in range(2)]
    WALL = [WX[h] + WG[h] + ["W%d.y" % h, "W%d.z" % h] for h in range(2)]

    dma("s", lambda g, T: g.sync.dma_start(T.SI[:], T.snd[:]), [], ["SI"], 1.8)
    dma("a", lambda g, T: g.scalar.dma_start(T.WIN0[:, 0:V], T.xa[:]), [], WX[0], 2.2)
    dma("s", lambda g, T: g.sync.dma_start(T.EI[:], T.ent[:]), [], ["EI"], 3.0)
    dma("a", lambda g, T: g.scalar.dma_start(T.UI[:], T.usr[:]), [], ["UI"], 3.6)
    dma("s", lambda g, T: g.sync.dma_start(T.TH8[:], T.th[:]), [], ["TH8"], 3.0)
    dma("s", lambda g, T: g.sync.dma_start(T.WIN0[:, 2048:4096], T.yc[:]), [], ["W0.y"], 4.5)
    dma("a", lambda g, T: g.scalar.dma_start(T.WIN1[:, 0:V], T.xa[:]), [], WX[1], 4.5)
    dma("s", lambda g, T: g.sync.dma_start(T.WIN1[:, 2048:4096], T.yc[:]), [], ["W1.y"], 5.5)
    dma("a", lambda g, T: g.scalar.dma_start(T.BN[:], T.bn[:]), [], ["BN"], 5.5)

    gp(lambda g, T: g.iota(T.CI[:], [[0, 2], [1, 4], [0, 8]], 0, 0), [], ["CI"], 128)
    vec(vts(buf("S4"), buf("SI"), 4, A.mult), ["SI"], ["S4"], 64)
    vec(vtt(buf("S5"), buf("S4"), buf("CI"), A.add), ["S4", "CI"], ["S5"], 128)
    vec(vcopy(buf("so4"), buf("S5")), ["S5"], ["so4"], 64)
    vec(lambda g, T: g.vector.tensor_copy(T.sI1[:], T.WIN0[:, 0:V].indirect(T.so4[:, 0:32])), ["so4"] + WX[0], ["sI1"], 60 + 512 * GC)
    act(lambda g, T: g.scalar.activation(T.sI2[:], T.WIN0[:, 0:V].indirect(T.so4[:, 32:64]), F.Copy), ["so4"] + WX[0], ["sI2"], 75 + 512 * GC)
    op("g", ("send", 0, "sI1", "sI2"), ["sI1", "sI2"], ["sent0"], 1.0)
    op("x", None, ["sent0"], WG[0], 0.0, 1, 5.0, "arr0")
    vec(vcopy(buf("su"), buf("SI")), ["SI"], ["su"], 64)

    vec(fill("ONE", 1.0), [], ["ONE"], 512)
    gp(lambda g, T: g.affine_select(cols(T, "BT"), T.ONE[:, 0:128], [[-16, 8], [0, 16]], A.is_ge, 0.0, 0, 1), ["ONE"], ["BT"], 256)
    gp(lambda g, T: g.affine_select(cols(T, "BLK"), cols(T, "BT"), [[16, 8], [0, 16]], A.is_ge, 0.0, 15, -1), ["BT"], ["BLK"], 256)
    gp(lambda g, T: g.iota(T.PI[:], [[1, 1]], 0, 1), [], ["PI"], 2)
    gp(lambda g, T: g.affine_select(cols(T, "ID"), T.ONE[:, 0:128], [[-1, 128]], A.is_equal, 0.0, 0, 1), ["ONE"], ["ID"], 256)
    gp(lambda g, T: g.iota(cols(T, "NROW"), [[1, 128]], 0, 0, allow_small_or_imprecise_dtypes=True), [], ["NROW"], 256)
    gp(lambda g, T: g.iota(cols(T, "KROW"), [[0, 8], [1, 16]], 0, 0, allow_small_or_imprecise_dtypes=True), [], ["KROW"], 256)
    vec(fill("O8", 1.0), [], ["O8"], 128)
    gp(lambda g, T: g.affine_select(T.B8T[0:8, :], T.O8[0:8, :], [[1, 128]], A.is_ge, 0.0, 0, -16), ["O8"], ["B8T"], 256)
    gp(lambda g, T: g.affine_select(T.B8[0:8, :], T.B8T[0:8, :], [[-1, 128]], A.is_ge, 0.0, 15, 16), ["B8T"], ["B8"], 256)
    vec(fill("RMX", 0.0), [], ["RMX"], 256)
    vec(fill("RMX", -1024.0, 0, 512, 16), [], ["RMX"], 64)
    act(aact(buf("RMN"), buf("RMX"), F.Copy, 0.0, -1.0), ["RMX"], ["RMN"], 512)
    vec(fill("RK", 0.0), [], ["RK"], 64)
    vec(fill("RK", 2097152.0, 0, 128, 16), [], ["RK"], 64)
    vec(fill("M25", -0.25, 0, 128), [], ["M25"], 64)
    vec(fill("MGC", MAGIC, 0, 128), [], ["MGC"], 64)
    vec(fill("O16", 1.0 / 16), [], ["O16"], 128)
    for h in range(2):
        vec(fill("KM%d" % h, 8388608.0, 128, 144), [], ["KMP%d" % h], 64)
    vec(fill("RS", 0.0), [], ["RS"], 64)
    vec(fill("RS", -16777216.0, 0, 256, 16), [], ["RS"], 64)
    vec(vts(buf("KI"), buf("PI"), 15, A.bitwise_and), ["PI"], ["KI"], 64)
    vec(vcopy(buf("KC"), buf("KI")), ["KI"], ["KC"], 64)
    vec(vts(buf("G16"), buf("BLK", 0, 128, 16), 16.0, A.mult), ["BLK"], ["G16"], 64)
    vec(vts(buf("CC", 0, 1), buf("KC"), 0.0, A.is_equal, 8.0, A.mult), ["KC"], ["CC0"], 64)
    vec(vts(buf("CC", 8, 9), buf("KC"), 1.0, A.is_equal), ["KC"], ["CC1"], 64)
    vec(vts(buf("CC", 18, 19), buf("KC"), 4.0, A.is_equal, -1168.0, A.mult), ["KC"], ["CC4"], 64)
    vec(vtt(buf("CC", 19, 20), buf("CC", 0, 1), buf("CC", 8, 9), A.add), ["CC0", "CC1"], ["CC3"], 64)
    vec(vtt(buf("CC", 16, 17), buf("CC", 18, 19), buf("CC", 19, 20), A.add), ["CC3", "CC4"], ["CC2"], 64)
    vec(vts(buf("BW"), buf("BLK"), buf("CC", 16, 17), A.mult), ["BLK", "CC2"], ["BW"], 64)
    vec(vts(buf("MAD"), buf("KROW"), buf("KC"), A.not_equal, -8388608.0, A.mult), ["KROW", "KC"], ["MAD"], 64)
    for h in range(2):
        act(aact(buf("V4%d" % h), buf("NROW"), F.Identity, 512.0 * h, 4.0), ["NROW"], ["V4%d" % h], 128)
    for j, (k, val) in enumerate(((2, 16384.0), (3, -8192.0), (4, -8192.0), (5, 4096.0), (5, 2048.0))):
        vec(vts(buf("CC", 24 + 8 * j, 25 + 8 * j), buf("KC"), float(k), A.is_equal, val, A.mult), ["KC"], ["CD%d" % j], 64)
    vec(vtt(buf("KR2"), buf("KROW"), buf("KROW"), A.mult), ["KROW"], ["KR2"], 256)
    vec(vts(buf("W1"), buf("KROW"), buf("CC", 24, 25), A.mult), ["KROW", "CD0"], ["W1"], 128)
    vec(vts(buf("W2"), buf("KR2"), buf("CC", 40, 41), A.mult, buf("CC", 32, 33), A.add), ["KR2", "CD1", "CD2"], ["W2"], 128)
    vec(vtt(buf("W3"), buf("W1"), buf("W2"), A.add), ["W1", "W2"], ["W3"], 256)
    vec(vts(buf("W4"), buf("W3"), buf("CC", 48, 49), A.add), ["W3", "CD3"], ["W4"], 128)
    vec(vts(buf("W5"), buf("W3"), -1.0, A.mult, buf("CC", 56, 57), A.add), ["W3", "CD4"], ["W5"], 128)
    vec(vtt(buf("WA"), buf("W4"), buf("BLK"), A.mult), ["W4", "BLK"], ["WA"], 256)
    vec(vtt(buf("WA2"), buf("W5"), buf("BLK"), A.mult), ["W5", "BLK"], ["WA2"], 256)
    vec(vts(buf("DK"), buf("ID"), buf("KC"), A.mult), ["ID", "KC"], ["DK"], 128)
    gp(lambda g, T: g.iota(T.PF[:], [[1, 1]], 0, 1, allow_small_or_imprecise_dtypes=True), [], ["PF"], 2)
    vec(vtt(buf("CC", 20, 21), buf("PF"), buf("KC"), A.subtract), ["PF", "KC"], ["CC5"], 64)
    vec(vts(buf("DG8"), buf("ID"), 16384.0, A.mult, buf("CC", 20, 21), A.mult), ["ID", "CC5"], ["DG8"], 128)
    for nm, val, src in (("IH", 0.5, "ID"), ("I64", 65536.0, "ID"), ("IBG", 1048576.0, "ID"), ("IM1", -1.0, "ID"), ("I2K", 2048.0, "ID"), ("IM16", -16.0, "ID"), ("IT1", 1.0, "ID"), ("IT2", 2.0, "ID"), ("IT3", 3.0, "ID"), ("BS", 1024.0, "BLK"), ("NBK", -8192.0, "BLK")):
        act(aact(buf(nm), buf(src), F.Copy, 0.0, val), [src], [nm], 128)
    vec(vcopy(buf("THF"), buf("TH8")), ["TH8"], ["THF"], 64)
    pe(mms([(buf("P30", 0, 4), lambda T: T.B8[0:8, :], lambda T: T.THF[:], True, True)]), ["B8", "THF"], ["P30"], 256, 1)
    vec(vcopy(buf("THC"), buf("P30", 0, 4)), ["P30"], ["THC"], 64)
    vec(vcopy(buf("THR", 0, 1), buf("THC", 0, 1)), ["THC"], ["THR"], 64)

    vec(vts(buf("dg0"), buf("UI"), 1.0 / 128, A.mult, 129.0 - 127.0 / 256, A.add), ["UI"], ["dg0"], 1024)
    vec(vts(buf("UT"), buf("UI"), 127, A.bitwise_and), ["UI"], ["UT"], 1024)
    vec(vcopy(buf("dgL"), buf("UT")), ["UT"], ["dgL"], 1024)
    vec(vts(buf("dg1"), buf("dgL"), 1.0 / 16, A.mult, 136.0 - 15.0 / 32, A.add), ["dgL"], ["dg1"], 512)
    for b in range(2):
        p = "P0%d" % b
        pe(mms([(buf(p), buf("ID"), buf("dgL", 512 * b, 512 * b + 512), True, False),
                (buf(p), buf("IM16"), buf("dg1", 512 * b, 512 * b + 512), False, True)]), ["ID", "IM16", "dgL", "dg1"], [p], 1024, 2)
        act(aact(buf("dg2", 512 * b, 512 * b + 512), buf(p), F.Identity, 2176.0), [p], ["dg2"], 512)
    act(aact(buf("dg3"), buf("dg2"), F.Square), ["dg2"], ["dg3"], 1024)

    def flat(d, src):
        return lambda g, T: g.sync.dma_start(T.Ud[d::16, :], T[src][:])
    for d in range(4, 16):
        dma("s", flat(d, "ONE"), ["ONE", "sent0"], ["Ud.%d" % d], 2.0 + 0.7 * (d - 3))
    for d in range(4):
        dma("s", flat(d, "dg%d" % d), ["dg%d" % d], ["Ud.%d" % d], 3.0)
    UDK = ["Ud.%d" % d for d in range(16)]
    EEK = ["EE.%d" % c for c in range(4)]
    vec(vcopy(buf("EE"), buf("EI")), ["EI"], EEK, 1024)

    def cls(t, h):
        return t + 512 * h, 512 * h + 512, 4

    def clean(t, h):
        a, b, s = cls(t, h)
        H = "%d" % h
        vec(vcopy(buf("EJ" + H), buf("EI", a, b, s)), ["EI"], ["EJ" + H], 128)
        act(aact(buf("PC" + H), buf("EE", a, b, s), F.Sign, -2047.5), ["EE.%d" % t], ["PC" + H], 128)
        pe(mms([(buf("P0" + H, 128, 256), buf("BLK"), buf("PC" + H), True, True)]), ["BLK", "PC" + H], ["P0" + H], 128, 1)
        act(aact(buf("%s%d" % ("NO" if t % 2 else "NP", h)), buf("P0" + H, 128, 256), F.Relu, -15.0), ["P0" + H], ["NO%d.%d" % (t % 2, h)], 128)

    def minus(t, h, c):
        a, pb = t + 512 * h + 128 * c, "P%d%d" % (BANK[c], h)
        for j in range(0, 16, 4):
            pe(mms([(buf(pb, k, 512, 16), buf("IM1"), buf("WIN0", a, a + 128 - t, 4), k == 0, False) for k in range(j, j + 4)]),
               ["IM1", "W0.x%d" % t], [pb], 256, 4)

    for h in range(2):
        clean(0, h)
        for c in range(4):
            minus(0, h, c)
    act(lambda g, T: g.scalar.activation(T.WIN1[:, 1024:2048], T.WIN0[:, 1024:2048], F.Copy), WG[0], WG[1], 1024)
    for h in range(2):
        vec(fill("WIN%d" % h, 0.0, 4096, 4224), [], ["W%d.z" % h], 64)

    def rounding(h, bank, out, outkey):
        H = "%d" % h
        act(aact(out, buf(bank, 0, 128), F.Abs, -MAGIC, 1.0), [bank], [outkey], 128)

    def scans(h, src, c, n, mx="MX", mn="MN"):
        H = "%d" % h
        a, b = n * c, n * c + n
        for dst, res, f in ((mx + H, "RMX", A.max), (mn + H, "RMN", A.min)):
            vec(lambda g, T, dst=dst, res=res, f=f: g.vector.tensor_tensor_scan(T[dst][:, a:b], T[res][:, 0:n], T[src][:, a:b], 0.0, A.add, f),
                [res, "%s.%d" % (src, c)], ["%s.%d" % (dst, c)], n // 2)

    def small(where, fout, fsrc, r, w):
        if where:
            act(lambda g, T: g.scalar.activation(fout(T), fsrc(T), F.Copy), r, w, 75 + 128 * GC)
        else:
            vec(lambda g, T: g.vector.tensor_copy(fout(T), fsrc(T)), r, w, 60 + 128 * GC)

    def fmm(h, bank, bsrc, bkey, mx="MX", mn="MN"):
        H = "%d" % h
        st = [(buf(bank, 0, 128), buf("ID"), buf("M25"), True, False), (buf(bank, 0, 128), buf("IM1"), bsrc, False, False)]
        rk = ["ID", "M25", "IM1", bkey]
        pe(mms(st), rk, [bank], 128 * len(st), len(st))
        kx, kn = [["%s%d.%d" % (m, h, c) for c in range(2048 // BCH)] for m in (mx, mn)]
        pe(mms([(buf(bank, 0, 128), buf("IH"), buf(mx + H, 15, 2048, 16), False, False)]), ["IH"] + kx, [bank], 128, 1)
        pe(mms([(buf(bank, 0, 128), buf("IH"), buf(mn + H, 15, 2048, 16), False, False),
                (buf(bank, 0, 128), buf("ID"), buf("MGC"), False, True)]), ["ID", "IH", "MGC"] + kn, [bank], 256, 2)

    def bulk(h, hop):
        H = "%d" % h
        for c in range(2048 // BCH):
            src = ind("WIN" + H, 0, WINW, "EO" + H, BCH // 16 * c, BCH // 16 * (c + 1))
            out = buf("G" + H, BCH * c, BCH * c + BCH)
            if PARAM["bulk"][hop][h][c]:
                act(lambda g, T, o=out, s=src: g.scalar.activation(o(T), s(T), F.Copy), WALL[h] + ["EO" + H], ["G%d.%d" % (h, c)], 75 + BCH * GC)
            else:
                vec(lambda g, T, o=out, s=src: g.vector.tensor_copy(o(T), s(T)), WALL[h] + ["EO" + H], ["G%d.%d" % (h, c)], 60 + BCH * GC)
        for c in range(2048 // BCH):
            scans(h, "G" + H, c, BCH)

    def diagonal(h, bank, a=0):
        H = "%d" % h
        vec(lambda g, T: g.vector.tensor_tensor_scan(cols(T, "LF" + H), T.RS[:, 0:128], T[bank][:, a:a + 128], 0.0, A.add, A.max),
            ["RS", bank], ["LF" + H], 128)

    for t in range(RO):
        for h in range(2):
            half[0] = h
            H = "%d" % h
            a, b, s = cls(t, h)
            for c in range(4):
                p, q, pb = 512 * c, 512 * c + 512, "P%d%s" % (BANK[c], H)
                src = ind("WIN" + H, 0, 4096, "EJ" + H, 32 * c, 32 * c + 32)
                rk, dk, ak = WALL[h][:-1] + ["EJ" + H], "D%d.%d" % (h, c), "AB%d.%d" % (h, c)
                if PARAM["judge"][h][c]:
                    act(lambda g, T, o=buf("D" + H, p, q), s=src: g.scalar.activation(o(T), s(T), F.Copy), rk, [dk], 75 + 512 * GC)
                else:
                    vec(lambda g, T, o=buf("D" + H, p, q), s=src: g.vector.tensor_copy(o(T), s(T)), rk, [dk], 60 + 512 * GC)
                pe(mms([(buf(pb), buf("ID"), buf("D" + H, p, q), False, True)]), ["ID", dk], [pb], 512, 1)
                act(aact(buf("AB" + H, p, q), buf(pb), F.Abs), [pb], [ak], 512)
            pe(mms([(buf("P0" + H, 0, 128), buf("PC" + H), buf("I64"), True, False),
                    (buf("P0" + H, 0, 128), buf("ONE", 0, 128), buf("DK"), False, False), (buf("P0" + H, 0, 128), buf("ONE", 0, 128), buf("DG8"), False, False)]),
               ["PC" + H, "I64", "ONE", "DK", "DG8"], ["P0" + H], 384, 3)
            pe(mms([(buf("P0" + H, k, 128, 16), buf("AB" + H, k, 2048, 16), buf("G16"), False, k == 15) for k in range(16)]),
               ["AB%d.%d" % (h, c) for c in range(4)] + ["G16"], ["P0" + H], 1024, 16)
            vec(lambda g, T, H=H: g.vector.tensor_tensor_scan(T["KM" + H][:, 0:128], cols(T, "RK"), T["P0" + H][:, 0:128], 0.0, A.add, A.min),
                ["RK", "P0" + H, "KMP" + H], ["KM" + H], 128)
            vec(lambda g, T, H=H: g.vector.tensor_tensor_scan(cols(T, "KE" + H), cols(T, "RK"), T["KM" + H][:, 15:143], 0.0, A.add, A.min),
                ["RK", "KM" + H, "KMP" + H], ["KE" + H], 128)
            vec(vtt(buf("HIT" + H), buf("P0" + H, 0, 128), buf("KE" + H), A.is_equal), ["P0" + H, "KE" + H], ["HIT" + H], 128)
            pe(mms([(buf("P1" + H, 0, 128), buf("HIT" + H), buf("I2K"), True, True)]), ["HIT" + H, "I2K"], ["P1" + H], 128, 1)
            vec(vtt(buf("E2" + H), buf("EI", a, b, s), buf("P1" + H, 0, 128), A.add), ["EI", "P1" + H], ["E2" + H], 128)
            vec(vts(buf("EO" + H), buf("E2" + H), 4095.0, A.min), ["E2" + H], ["EO" + H], 128)
            if t < RO - 1:
                clean(t + 1, h)
            for c in range(2048 // BCH):
                scans(h, "D" + H, c, BCH, "MF", "NF")
            fmm(h, "P2" + H, buf("BN", a, b, s), "BN", "MF", "NF")
            rounding(h, "P2" + H, buf("F0" + H), "F0" + H)
            bulk(h, 0)
            fmm(h, "P3" + H, buf("BN", a, b, s), "BN")
            rounding(h, "P3" + H, buf("WIN" + H, 4096, 4224), "W%d.z" % h)
            rounding(h, "P3" + H, buf("Z0" + H), "Z0" + H)
            for hop in (1, 2):
                p0 = buf("P0" + H, 0, 128)
                st, rk = [(p0, buf("ID"), buf("MAD"), True, False)], ["ID", "MAD"]
                if hop == 1:
                    st.append((p0, buf("ID"), buf("V4%d" % h), False, False))
                    rk.append("V4%d" % h)
                    if t:
                        st.append((p0, buf("IT%d" % t), buf("ONE", 0, 128), False, False))
                        rk += ["IT%d" % t, "ONE"]
                else:
                    st.append((p0, buf("BW"), buf("DG" + H), False, False))
                    rk += ["BW", "DG" + H]
                pe(mms(st), rk, ["P0" + H], 128 * len(st), len(st))
                pe(mms([(p0, buf("BS"), buf("WIN" + H, 4096, 4224), False, True)]), ["BS", "W%d.z" % h], ["P0" + H], 128, 1)
                diagonal(h, "P0" + H)
                vec(vcopy(buf("SLI" + H), buf("LF" + H, 15, 128, 16)), ["LF" + H], ["SLI" + H], 64)
                vec(vts(buf("SLA" + H), buf("SLI" + H), 16383, A.bitwise_and), ["SLI" + H], ["SLA" + H], 64)
                vec(vcopy(buf("SLO" + H), buf("SLA" + H)), ["SLA" + H], ["SLO" + H], 64)
                small(PARAM["dg"][hop - 1][h], buf("DG" + H), ind("Ud", 0, 16384, "SLO" + H, 0, 8), UDK + ["SLO" + H], ["DG" + H])
                pe(mms([(buf("P1" + H, 0, 128), buf("ID"), buf("MAD"), True, False)]), ["ID", "MAD"], ["P1" + H], 128, 1)
                pe(mms([(buf("P1" + H, 0, 128), buf("BW"), buf("DG" + H), False, True)]), ["BW", "DG" + H], ["P1" + H], 128, 1)
                pe(mms([(buf("P2" + H, 0, 128), buf("ID"), buf("NROW"), True, False), (buf("P2" + H, 0, 128), buf("WA"), buf("DG" + H), False, True),
                        (buf("P2" + H, 128, 256), buf("WA2"), buf("DG" + H), True, True)]), ["ID", "NROW", "WA", "WA2", "DG" + H], ["P2" + H], 384, 3)
                diagonal(h, "P1" + H)
                vec(vcopy(buf("WLO" + H), buf("LF" + H, 15, 128, 16)), ["LF" + H], ["WLO" + H], 64)
                act(aact(buf("AA" + H, 0, 256), buf("P2" + H, 0, 256), F.Copy), ["P2" + H], ["AA" + H], 256)
                eg = ind("EE", 0, 1024, "WLO" + H, 0, 8)
                vec(vtt(buf("E2" + H), eg, buf("AA" + H, 0, 128), A.max), EEK + ["WLO" + H, "AA" + H], ["E2" + H], 60 + 128 * GC)
                vec(vcopy(buf("EO" + H), buf("E2" + H)), ["E2" + H], ["EO" + H], 128)
                act(lambda g, T, H=H: g.scalar.activation(T["BG" + H][:], T.BN[:, 0:1024].indirect(T["WLO" + H][:, 0:8]), F.Copy),
                    ["BN", "WLO" + H], ["BG" + H], 75 + 128 * GC)
                if hop == 2:
                    act(lambda g, T, H=H: g.scalar.activation(T["XG" + H][:], T["WIN" + H][:, 0:1024].indirect(T["WLO" + H][:, 0:8]), F.Copy),
                        WX[h] + ["WLO" + H], ["XG" + H], 75 + 128 * GC)
                vec(vtt(buf("DD%d%d" % (hop, h)), eg, buf("AA" + H, 128, 256), A.is_ge), EEK + ["WLO" + H, "AA" + H], ["DD%d%d" % (hop, h)], 60 + 128 * GC)
                bulk(h, hop)
                fmm(h, "P3" + H, buf("BG" + H), "BG" + H)
                rounding(h, "P3" + H, buf("WIN" + H, 4096, 4224), "W%d.z" % h)
            pe(mms([(buf("P3" + H, 0, 128), buf("IM1"), buf("XG" + H), True, False)]), ["IM1", "XG" + H], ["P3" + H], 128, 1)
            pe(mms([(buf("P3" + H, 0, 128), buf("ID"), buf("WIN" + H, 4096, 4224), False, True)]), ["ID", "W%d.z" % h], ["P3" + H], 128, 1)
            act(aact(buf("AD" + H), buf("P3" + H, 0, 128), F.Abs), ["P3" + H], ["AD" + H], 128)
            pe(mms([(buf("P2" + H, 0, 128), buf("ID"), buf("Z0" + H), True, False), (buf("P2" + H, 0, 128), buf("IM1"), buf("F0" + H), False, True),
                    (buf("P2" + H, 128, 256), buf("HIT" + H), buf("I2K"), True, True), (buf("P2" + H, 384, 512), buf("ID"), buf("F0" + H), True, True)]),
               ["ID", "IM1", "I2K", "Z0" + H, "F0" + H, "HIT" + H], ["P2" + H], 512, 4)
            pe(mms([(buf("P1" + H, 0, 128), buf("IBG"), buf(("NO" if t % 2 else "NP") + H), True, False), (buf("P1" + H, 0, 128), buf("NBK"), buf("DD1" + H), False, False),
                    (buf("P1" + H, 0, 128), buf("NBK"), buf("DD2" + H), False, False)]), ["IBG", "NO%d.%d" % (t % 2, h), "NBK", "DD1" + H, "DD2" + H], ["P1" + H], 384, 3)
            pe(mms([(buf("P1" + H, 0, 128), buf("BLK"), buf("AD" + H), False, True)]), ["BLK", "AD" + H], ["P1" + H], 128, 1)
            vec(vts(buf("ST" + H), buf("P1" + H, 0, 128), buf("THR", t, t + 1), A.is_le), ["P1" + H, "THR"], ["ST" + H], 128)
            vec(vtt(buf("SX" + H), buf("ST" + H), buf("P2" + H, 0, 128), A.mult), ["ST" + H, "P2" + H], ["SX" + H], 128)
            vec(vtt(buf("XN", 128 * h, 128 * h + 128), buf("P2" + H, 384, 512), buf("SX" + H), A.add), ["P2" + H, "SX" + H], ["XN.%d" % h], 128)
        half[0] = 1
        XNK = ["XN.0", "XN.1"]
        if t < RO - 1:
            vec(lambda g, T, t=t: g.vector.tensor_copy(cols(T, "sa%d" % t), T.XN[:, 0:256].indirect(T.su[:, 8 * t:8 * t + 8])), XNK + ["su"], ["sa%d" % t], 60 + 128 * GC)
            act(lambda g, T, t=t: g.scalar.activation(cols(T, "sb%d" % t), T.XN[:, 0:256].indirect(T.su[:, 8 * t + 32:8 * t + 40]), F.Copy), XNK + ["su"], ["sb%d" % t], 75 + 128 * GC)
            op("g", ("send", t + 1, "sa%d" % t, "sb%d" % t), ["sa%d" % t, "sb%d" % t], ["sent%d" % (t + 1)], 0.6)
            op("x", None, ["sent%d" % (t + 1)], ["la%d" % t], 0.0, 1, 2.5, "arr%d" % (t + 1))
            act(aact(buf("WIN1", t, 1024, 4), buf("XN"), F.Copy), XNK, ["W1.x%d" % t], 256)
        vec(vcopy(buf("WIN0", t, 1024, 4), buf("XN")), XNK, ["W0.x%d" % t], 128)
        if t == RO - 1:
            dma("s", lambda g, T: g.sync.dma_start(T.yx[:], T.WIN0[:, 0:V]), WX[0], [], 2.0)
        for h in range(2):
            H = "%d" % h
            a, b, s = cls(t, h)
            vec(vtt(buf("SH" + H), buf("ST" + H), buf("P2" + H, 128, 256), A.mult), ["ST" + H, "P2" + H], ["SH" + H], 128)
            pe(mms([(buf("P2" + H, 256, 384), buf("ID"), buf("SH" + H), True, True)]), ["ID", "SH" + H], ["P2" + H], 128, 1)
            vec(vtt(buf("EE", a, b, s), buf("EI", a, b, s), buf("P2" + H, 256, 384), A.add), ["EI", "P2" + H], ["EE.%d" % t], 128)
        if t == RO - 1:
            dma("a", lambda g, T: g.scalar.dma_start(T.ye[:], T.EE[:]), EEK, [], 2.0)
        else:
            for h in range(2):
                H = "%d" % h
                act(lambda g, T, H=H, h=h: g.scalar.activation(cols(T, "AD" + H), cols(T, "ST" + H), F.Copy, accum_out=T.CNT[:, h:h + 1]),
                    ["ST" + H], ["CNT", "AD" + H], 150)
            pe(mms([(buf("P20", 384, 386), buf("O16"), buf("CNT"), True, True)]), ["O16", "CNT"], ["P20"], 256, 1)
            vec(vcopy(buf("W1", 0, 2), buf("P20", 384, 386)), ["P20"], ["W1"], 64)
            vec(vtt(buf("RI"), buf("W1", 0, 1), buf("W1", 1, 2), A.add), ["W1"], ["RI"], 64)
            vec(vts(buf("RA"), buf("RI"), 31, A.bitwise_and), ["RI"], ["RA"], 64)
            vec(vtt(buf("THR", t + 1, t + 2), buf("THC", t + 1, t + 2), buf("RA"), A.add), ["THC", "RA"], ["THR"], 64)
            for c in range(4):
                for h in range(2):
                    minus(t + 1, h, c)
            for h in range(2):
                for n in range(2):
                    a = 1024 + 512 * n + 128 * t
                    o, i = buf("WIN%d" % h, a, a + 128), buf("la%d" % t, 128 * n, 128 * n + 128)
                    if n:
                        act(aact(o, i, F.Copy), ["la%d" % t], ["W%d.g%d" % (h, n)], 128)
                    else:
                        vec(vcopy(o, i), ["la%d" % t], ["W%d.g%d" % (h, n)], 64)
    return ops


SEMQ = {"v": "cv", "a": "ca", "p": "cp", "g": "cg"}


def is_psum(k):
    return len(k) == 3 and k[0] == "P" and k[1] in "0123" and k[2] in "01"


def link(ops):
    lw, rd = {}, {}
    pred = []
    for o in ops:
        p = {}
        i = o["i"]

        def add(j, wait):
            p[j] = p.get(j, False) or wait
        for k in o["after"]:
            if k in lw:
                add(lw[k], False)
        for k in o["r"]:
            if k in lw:
                add(lw[k], True)
            if is_psum(k):
                for j in rd.get(k, []):
                    if ops[j]["q"] != o["q"]:
                        add(j, True)
        for k in o["w"]:
            if k in lw:
                j = lw[k]
                add(j, not (o["q"] == "p" and ops[j]["q"] == "p"))
            for j in rd.get(k, []):
                add(j, not (o["q"] == "p" and ops[j]["q"] == "p"))
        for k in o["r"]:
            rd.setdefault(k, []).append(i)
        for k in o["w"]:
            lw[k] = i
            rd[k] = []
        p.pop(i, None)
        pred.append(p)
    return pred


def schedule(ops, pred):
    n = len(ops)
    succ = [[] for _ in range(n)]
    for i in range(n):
        for j in pred[i]:
            succ[j].append(i)
    LAT = SLAT
    prio = [0.0] * n
    for i in range(n - 1, -1, -1):
        o = ops[i]
        prio[i] = o["cost"] + o["lat"] + max([prio[k] + LAT for k in succ[i]], default=0.0)
    for i in range(n):
        o = ops[i]
        if o["h"] == 0:
            prio[i] += AHEAD
        if o["w"] and o["w"][0][:2] in BULK:
            prio[i] -= BULK[o["w"][0][:2]]
        if o["w"]:
            prio[i] += PRIO.get(o["q"] + o["w"][0], 0.0)
    best = forward(ops, pred, succ, prio)
    res, stale = best, 0
    for _ in range(PASSES):
        late = backward(ops, pred, succ, res)
        res = forward(ops, pred, succ, [-x for x in late])
        if max(res[2]) < max(best[2]) - 1e-9:
            best = res
    return best


def backward(ops, pred, succ, res):
    n = len(ops)
    fin = res[2]
    left = [len(succ[i]) for i in range(n)]
    at, free, late, done = [0.0] * n, {}, [0.0] * n, 0
    ready = {}
    for i in range(n):
        if left[i] == 0:
            ready.setdefault(ops[i]["q"], []).append(i)
    while done < n:
        best = None
        for q, lst in ready.items():
            if not lst:
                continue
            s = max(free.get(q, 0.0), min(at[i] for i in lst))
            i = max((i for i in lst if at[i] <= s + 1e-9), key=lambda i: (fin[i], i))
            if best is None or s < best[0]:
                best = (s, q, i)
        s, q, i = best
        ready[q].remove(i)
        e = s + ops[i]["cost"]
        free[q] = e if q != "x" else 0.0
        late[i] = -e
        done += 1
        for j in pred[i]:
            at[j] = max(at[j], e + (SLAT if pred[i][j] else 0.0) + ops[j]["lat"])
            left[j] -= 1
            if left[j] == 0:
                ready.setdefault(ops[j]["q"], []).append(j)
    return late


def forward(ops, pred, succ, prio):
    n = len(ops)
    LAT = SLAT
    left = [len(pred[i]) for i in range(n)]
    ready = {}
    at = [0.0] * n
    free = {}
    order, fin = [], [0.0] * n
    for i in range(n):
        if left[i] == 0:
            ready.setdefault(ops[i]["q"], []).append(i)
    start = [0.0] * n
    while len(order) < n:
        best = None
        for q, lst in ready.items():
            if not lst:
                continue
            f = free.get(q, 0.0)
            s = max(f, min(at[i] for i in lst))
            j = max((i for i in lst if at[i] <= s + WINDOW), key=lambda i: (prio[i], -i))
            if at[j] > s + 1e-9:
                fit = [i for i in lst if at[i] <= s + 1e-9 and s + ops[i]["cost"] <= at[j] + SLACK * ops[i]["cost"]]
                if fit:
                    i = max(fit, key=lambda i: (prio[i], -i))
                else:
                    i, s = j, at[j]
            else:
                i = j
            if best is None or s < best[0]:
                best = (s, q, i)
        s, q, i = best
        ready[q].remove(i)
        o = ops[i]
        start[i] = s
        free[q] = s + (o["cost"] if q != "x" else 0.0)
        fin[i] = s + o["cost"] + o["lat"]
        order.append(i)
        for k in succ[i]:
            wt = pred[k][i]
            at[k] = max(at[k], fin[i] + (LAT if wt else 0.0))
            left[k] -= 1
            if left[k] == 0:
                ready.setdefault(ops[k]["q"], []).append(k)
    return order, start, fin


CACHE = {}


def plan():
    if "p" not in CACHE:
        ops = build()
        pred = link(ops)
        order, start, fin = schedule(ops, pred)
        place = {i: k for k, i in enumerate(order)}
        pos = {}
        tot = {}
        know = {}
        seen = {}
        prog = []
        for i in order:
            o = ops[i]
            q = o["q"]
            kn = dict(seen.get(q, {}))
            waits = []
            need = {}
            for j, wt in pred[i].items():
                if not wt:
                    continue
                sem, val = pos[j]
                if sem is not None and val > need.get(sem, 0):
                    need[sem] = val
            for j in sorted(pred[i], key=lambda j: -place[j]):
                if not pred[i][j]:
                    continue
                sem, val = pos[j]
                if sem is None or kn.get(sem, 0) >= val:
                    continue
                waits.append((sem, need[sem]))
                kn[sem] = max(kn.get(sem, 0), need[sem])
                for s2, v2 in know[j].items():
                    kn[s2] = max(kn.get(s2, 0), v2)
            seen[q] = kn
            kj = dict(kn)
            if o["sem"] is not None:
                pos[i] = (o["sem"], -1 if q == "x" else 16)
                kj[o["sem"]] = 16 if q != "x" else 1
                if q == "x":
                    pos[i] = (o["sem"], 1)
            elif isinstance(o["fn"], tuple):
                pos[i] = (None, 0)
            else:
                sm = SEMQ[q]
                tot[sm] = tot.get(sm, 0) + o["n"]
                pos[i] = (sm, tot[sm])
                kj[sm] = tot[sm]
            know[i] = kj
            prog.append((o, waits))
        CACHE["p"] = (prog, tot, ops, order, start, fin)
    return CACHE["p"]


def engines_of(core, d1, d2, topo):
    e1, e2 = topo.engines(core, d1), topo.engines(core, d2)
    both = [e for e in e1 if e in e2]
    only1, only2 = [e for e in e1 if e not in e2], [e for e in e2 if e not in e1]
    if only1:
        return only1, e2
    if only2:
        return e1, only2
    return both[:len(both) // 2], both[len(both) // 2:]


def bits(es):
    return sum(1 << e for e in es)


def rank_program(g, core, T, topo):
    rank = T.rank_of(core)
    if rank is None:
        return
    prog, tot, ops, order, start, fin = plan()
    n = len(T.cores)
    dst = [T.cores[(rank - k) % n] for k in (1, 2)]
    for d in dst:
        assert topo.may_write(core, d)
    masks = engines_of(core, dst[0], dst[1], topo)
    arrive = 0
    for k in (1, 2):
        c = T.cores[(rank + k) % n]
        m = engines_of(c, T.cores[(rank + k - 1) % n], T.cores[(rank + k - 2) % n], topo)
        arrive += len(m[k - 1])
    queue = {"v": g.vector, "a": g.scalar, "p": g.tensor, "g": g, "s": g.sync}
    sent = 0
    arrs = {"arr%d" % k: arrive for k in range(4)}
    for o, waits in prog:
        q = o["q"]
        if q == "x":
            continue
        for sem, val in waits:
            queue[q].wait_ge(T.sem[sem], arrs.get(sem, val))
        fn = o["fn"]
        if isinstance(fn, tuple):
            x = fn[1]
            tr = []
            for k in range(2):
                rid, pid, _ = topo.addr(dst[k])
                if x == 0:
                    land = T.WIN0[:, 1024 + 512 * k:1536 + 512 * k]
                else:
                    land = T["la%d" % (x - 1)][:, 128 * k:128 * k + 128]
                tr.append(RemoteDMATransfer(dst_ids=[DstId(rid=rid, pnc=pid)], dma_engine_mask=bits(masks[k]),
                                            remote_sem=T.sem["arr%d" % x], src=cols(T, fn[2 + k]), dst=land))
            g.remote_dma_fused(tr, local_sem=T.sem.loc)
            sent += len(masks[0]) + len(masks[1])
            continue
        r = fn(g, T)
        if o["sem"] is not None:
            r.then_inc(T.sem[o["sem"]], 16)
        elif isinstance(r, list):
            for x in r:
                x.then_inc(T.sem[SEMQ[q]], 1)
        else:
            r.then_inc(T.sem[SEMQ[q]], 1)
    for sem, val in tot.items():
        g.wait_ge(T.sem[sem], val)
    for o in ops:
        if o["sem"] is not None:
            g.wait_ge(T.sem[o["sem"]], arrs.get(o["sem"], 16))
    g.wait_ge(T.sem.loc, sent)
